import numpy as np
import ml_dtypes


def mxq(x, axis, fmt="e4m3"):
    dtype, down = {"e4m3": (ml_dtypes.float8_e4m3fn, 7), "e5m2": (ml_dtypes.float8_e5m2, 14)}[fmt]
    v = np.moveaxis(np.asarray(x, np.float32).astype(ml_dtypes.bfloat16).astype(np.float64), axis, -1)
    blocks = v.reshape(v.shape[:-1] + (-1, 32))
    amax = np.abs(blocks).max(-1, keepdims=True)
    byte = np.maximum(np.where(amax > 0, np.frexp(amax)[1] - 1 + 127, 0) - down, 1)
    scale = np.exp2(byte - 127.0)
    codes = (blocks / scale).astype(np.float32).astype(dtype).astype(np.float64)
    return np.moveaxis((codes * scale).reshape(v.shape), -1, axis)


WIDE = False


def mx_kscale(k):
    if not WIDE:
        return np.ones(k)
    levels = np.array([10, -10, 5, -5, 0])
    if k % 512:
        return np.exp2(np.random.permutation(np.resize(levels, k // 32))).repeat(32)
    a = np.empty((k // 512, 16))
    for p in range(k // 512):
        a[p, :8] = np.random.permutation(np.resize(levels, 8))
        for g in range(8):
            far = levels[np.abs(levels - a[p, g]) >= 10]
            a[p, g + 8] = far[np.random.randint(len(far))]
    return np.exp2(a.ravel()).repeat(32)


def f64(x):
    return np.asarray(x).astype(np.float64)


def striped(idx):
    return np.tile(idx.reshape(-1, 16).T, (8, 1)).astype(np.uint16)


def unstriped(offs):
    return offs[:16].T.reshape(-1).astype(np.int64)


def pack_weight(w):
    k, n = w.shape
    w = f64(np.asarray(w, np.float32).astype(ml_dtypes.bfloat16)).reshape(k // 32, 32, n)
    amax = np.abs(w).max(1)
    byte = np.clip(np.where(amax > 0, np.frexp(amax)[1] - 1 + 127 - 7, 1), 1, 254)
    scaled = (w * np.exp2(127.0 - byte)[:, None, :]).reshape(k, n).astype(np.float32)
    words = np.ascontiguousarray(scaled.reshape(k // 512, 128, 4, n).transpose(0, 1, 3, 2)).astype(ml_dtypes.float8_e4m3fn).view(np.uint8)
    return words, np.ascontiguousarray(byte.astype(np.uint8).reshape(k // 512, 16, n))


def unpack_weight(words, scales):
    g, p, n, _ = words.shape
    vals = np.ascontiguousarray(words).view(ml_dtypes.float8_e4m3fn).astype(np.float64) * np.repeat(np.exp2(scales.astype(np.float64) - 127.0), 8, axis=1)[..., None]
    return vals.transpose(0, 1, 3, 2).reshape(g * 512, n)


E2M1 = np.array([0.0, 0.5, 1.0, 1.5, 2.0, 3.0, 4.0, 6.0, -0.0, -0.5, -1.0, -1.5, -2.0, -3.0, -4.0, -6.0])


def pack_fp4(w):
    k, n = w.shape
    w = f64(np.asarray(w, np.float32).astype(ml_dtypes.bfloat16)).reshape(k // 32, 32, n)
    amax = np.abs(w).max(1)
    mant, ex = np.frexp(amax / 6.0)
    byte = np.clip(np.where(amax > 0, np.where(mant > 0.5, ex, ex - 1) + 127, 1), 1, 254)
    scaled = (w * np.exp2(127.0 - byte)[:, None, :]).reshape(k, n).astype(np.float32)
    c = np.ascontiguousarray(scaled.reshape(k // 512, 128, 4, n).transpose(0, 1, 3, 2)).astype(ml_dtypes.float4_e2m1fn).view(np.uint8) & 0xF
    words = (c[..., 0::2] | (c[..., 1::2] << 4)).reshape(k // 512, 128, 2 * n)
    return np.ascontiguousarray(words), np.ascontiguousarray(byte.astype(np.uint8).reshape(k // 512, 16, n))


def unpack_fp4(words, scales):
    g, _, n = scales.shape
    words = np.ascontiguousarray(words).reshape(g, 128, n, 2)
    nib = np.empty((g, 128, n, 4), np.uint8)
    nib[..., 0::2] = words & 0xF
    nib[..., 1::2] = words >> 4
    vals = E2M1[nib] * np.repeat(np.exp2(scales.astype(np.float64) - 127.0), 8, axis=1)[..., None]
    return vals.transpose(0, 1, 3, 2).reshape(g * 512, n)


def silu(v):
    return v / (1.0 + np.exp(-np.maximum(v, -700.0)))


K, T, S, V, H, N, J, U = 1024, 2048, 512, 256, 512, 256, 512, 512


def setup_inputs():
    n = np.random.standard_normal
    s = mx_kscale(K)[:, None]
    u = mx_kscale(H)
    r = mx_kscale(J)[:, None]
    packed_xT = pack_weight(n((K, T)) * s)
    packed_w2 = pack_fp4(n((H, N)) / np.sqrt(2 * H) / u[:, None])
    return {
        "x_words": packed_xT[0],
        "x_scales": packed_xT[1],
        "aT": (n((J, U)) * r).astype(np.float32),
        "w1": (n((K, H)) / np.sqrt(K) / s * u).astype(np.float32),
        "w3": (n((J, H)) / np.sqrt(J) / r).astype(np.float32),
        "w2_words": packed_w2[0],
        "w2_scales": packed_w2[1],
        "offs": striped(np.random.permutation(T)[:S]),
        "pos1": striped(np.random.permutation(S)[:V]),
        "pos2": striped(np.random.permutation(S)[:V]),
    }


def reference(x_words, x_scales, aT, w1, w3, w2_words, w2_scales, offs, pos1, pos2):
    xq = unpack_weight(x_words, x_scales)[:, unstriped(offs)]
    h = silu(mxq(f64(w1), 0, "e4m3").T @ xq)
    f = mxq(f64(w3), 0, "e4m3").T @ mxq(f64(aT), 0, "e4m3")
    z = h[:, unstriped(pos1)] * f[:, :V] + h[:, unstriped(pos2)] * f[:, V:2 * V]
    return silu(unpack_fp4(w2_words, w2_scales).T @ mxq(z, 0, "e4m3"))

@@ -1,0 +1,190 @@
+from contextlib import ExitStack
+
+import concourse.mybir as mybir
+
+K, T, S, V, H, N, J = 1024, 2048, 512, 256, 512, 256, 512
+FLOPS = 2 * K * H * S + 2 * J * H * 2 * V + 2 * H * N * V
+
+F32 = mybir.dt.float32
+BF16 = mybir.dt.bfloat16
+I32 = mybir.dt.int32
+U32 = mybir.dt.uint32
+U16 = mybir.dt.uint16
+U8 = mybir.dt.uint8
+FP8X4 = mybir.dt.float8_e4m3fn_x4
+FP4X4 = mybir.dt.float4_e2m1fn_x4
+SILU = mybir.ActivationFunctionType.Silu
+MULT = mybir.AluOpType.mult
+ADD = mybir.AluOpType.add
+
+P = 128
+W1_VECTOR_ROWS = 96
+
+
+def tile_picked_dime_silu_p_kernel(
+    tc, x_words, x_scales, aT, w1, w3, w2_words, w2_scales, offs, pos1, pos2, out
+):
+    nc = tc.nc
+    with ExitStack() as ctx:
+        sb = ctx.enter_context(tc.tile_pool(name="sb", bufs=1))
+        ps = ctx.enter_context(tc.psum_pool(name="ps", bufs=1))
+
+        def tile(name, shape, dtype):
+            return sb.tile(shape, dtype, name=name, align_bytes=64)
+
+        offs_t = tile("offs_t", [P, S // 16], U16)
+        pos_t = [tile("pos1_t", [P, V // 16], U16), tile("pos2_t", [P, V // 16], U16)]
+        xw = [tile("xw%d" % z, [P, T], I32) for z in range(2)]
+        xs = tile("xs", [P, T], U8)
+        w1_raw = [tile("w1_raw%d" % z, [P, 4, H], F32) for z in range(2)]
+        w3_raw = [tile("w3_raw%d" % u, [P, 4, H // 2], F32) for u in range(2)]
+        a_raw = [tile("a_raw%d" % u, [P, 4, V], F32) for u in range(2)]
+        w2w = tile("w2w", [P, 2 * N], U8)
+        w2s = tile("w2s", [P, N], U8)
+
+        warm = tile("warm", [P, 8], F32)
+        nc.gpsimd.memset(warm[:], 0.0)
+        warm2 = tile("warm2", [P, 8], F32)
+        nc.scalar.activation(warm2[:], warm[:], SILU)
+
+        nc.gpsimd.memset(xs[:].bitcast(I32), 0)
+        nc.gpsimd.memset(w2s[:].bitcast(I32), 0)
+        for q in range(4):
+            nc.gpsimd.dma_start(xs[32 * q : 32 * q + 8, :].bitcast(I32), x_scales[:, 4 * q : 4 * q + 4, :].bitcast(I32))
+        for q in range(4):
+            nc.gpsimd.dma_start(w2s[32 * q : 32 * q + 4, :].bitcast(I32), w2_scales[0, 4 * q : 4 * q + 4, :].bitcast(I32))
+
+        def load_x(z):
+            nc.sync.dma_start(xw[z][:], x_words[z].rearrange("p c r -> p (c r)").bitcast(I32))
+
+        def rows4(w):
+            return w.rearrange("(p j) c -> p j c", j=4)
+
+        nc.sync.dma_start(w1_raw[0][:], rows4(w1[0:512, :]))
+        nc.sync.dma_start(offs_t[:], offs)
+        load_x(0)
+        nc.sync.dma_start(w1_raw[1][:], rows4(w1[512:1024, :]))
+        load_x(1)
+        nc.sync.dma_start(w3_raw[0][:], rows4(w3[:, 0:256]))
+        nc.sync.dma_start(pos_t[0][:], pos1)
+        nc.sync.dma_start(pos_t[1][:], pos2)
+        nc.sync.dma_start(w3_raw[1][:], rows4(w3[:, 256:512]))
+        nc.sync.dma_start(a_raw[0][:], rows4(aT[:, 0:V]))
+        nc.sync.dma_start(a_raw[1][:], rows4(aT[:, V : 2 * V]))
+        nc.sync.dma_start(w2w[:], w2_words[0])
+
+        def deal(engine_copy, grouped, raw, m0, m1, raw_m0):
+            dst = grouped[:].rearrange("p (t m j) -> p m j t", t=4, j=4)[:, m0:m1]
+            src = raw[:].rearrange("p j (m t) -> p m j t", t=4)[:, m0 - raw_m0 : m1 - raw_m0]
+            engine_copy(dst, src)
+
+        def quant(name, grouped, width):
+            codes = tile(name + "_c", [P, width], U32)
+            scales = tile(name + "_s", [P, width], U8)
+            nc.vector.quantize_mx(out=codes[:].bitcast(FP8X4), scales=scales[:], in_=grouped[:])
+            return codes, scales
+
+        w1_g = [tile("w1_g%d" % z, [P, 4 * H], BF16) for z in range(2)]
+        w3_g = tile("w3_g", [P, 4 * H], BF16)
+        a_g = [tile("a_g%d" % u, [P, 4 * V], BF16) for u in range(2)]
+        xg = [tile("xg%d" % z, [P, S], U32) for z in range(2)]
+        xsg = tile("xsg", [P, S], U8)
+        h_ps = [ps.tile([P, S], F32, name="h_ps%d" % t) for t in range(4)]
+
+        def h_pass(z, codes, scales, t):
+            nc.tensor.matmul_mx(
+                out=h_ps[t][:],
+                lhsT=codes[:, t * P : (t + 1) * P].bitcast(FP8X4),
+                lhsT_scale=scales[:, t * P : (t + 1) * P],
+                rhs=xg[z][:].bitcast(FP8X4),
+                rhs_scale=xsg[4 * z : P, :],
+                start=(z == 0),
+                stop=(z == 1),
+            )
+
+        deal(nc.scalar.copy, w1_g[0], w1_raw[0], 0, P, 0)
+        nc.vector.tensor_copy(xg[0][:], xw[0][:].bitcast(U32).indirect(offs_t[:]))
+        c0, s0 = quant("w1a", w1_g[0], H)
+        nc.vector.tensor_copy(xsg[:], xs[:].indirect(offs_t[:]))
+        for t in range(4):
+            h_pass(0, c0, s0, t)
+        deal(nc.vector.tensor_copy, w1_g[1], w1_raw[1], 0, W1_VECTOR_ROWS, 0)
+        deal(nc.scalar.copy, w1_g[1], w1_raw[1], W1_VECTOR_ROWS, P, 0)
+        c1, s1 = quant("w1b", w1_g[1], H)
+        nc.vector.tensor_copy(xg[1][:], xw[1][:].bitcast(U32).indirect(offs_t[:]))
+        h = [tile("h%d" % t, [P, S], F32) for t in range(4)]
+        for t in range(4):
+            h_pass(1, c1, s1, t)
+            nc.scalar.activation(h[t][:], h_ps[t][:], SILU)
+        deal(nc.vector.tensor_copy, w3_g, w3_raw[0], 0, 64, 0)
+        deal(nc.scalar.copy, w3_g, w3_raw[1], 64, P, 64)
+
+        def weave(u):
+            dst = a_g[u][:].rearrange("p (c i j) -> p c j i", i=4, j=4)
+            src = a_raw[u][:].rearrange("p j (c i) -> p c j i", i=4)
+            nc.scalar.copy(dst, src)
+
+        weave(0)
+        weave(1)
+
+        g = [tile("g%d" % u, [P, 4, V], F32) for u in range(2)]
+
+        def fetch(u, t):
+            nc.vector.tensor_copy(g[u][:, t, :], h[t][:].indirect(pos_t[u][:]))
+
+        f_ps = [[ps.tile([P, 2, V], F32, name="f_ps%d%d" % (u, b)) for b in range(2)] for u in range(2)]
+
+        def f_product(u, wc, ws, ac, asc):
+            for t in range(4):
+                nc.tensor.matmul_mx(
+                    out=f_ps[u][t // 2][:, t % 2, :],
+                    lhsT=wc[:, t * P : (t + 1) * P].bitcast(FP8X4),
+                    lhsT_scale=ws[:, t * P : (t + 1) * P],
+                    rhs=ac[:].bitcast(FP8X4),
+                    rhs_scale=asc[:],
+                    start=True,
+                    stop=True,
+                )
+
+        for t in range(4):
+            fetch(0, t)
+        fetch(1, 0)
+        c3, s3 = quant("w3", w3_g, H)
+        fetch(1, 1)
+        fetch(1, 2)
+        ca, sa = quant("a0", a_g[0], V)
+        f_product(0, c3, s3, ca, sa)
+        fetch(1, 3)
+        m = [tile("m%d" % u, [P, 4, V], F32) for u in range(2)]
+
+        def times(u, b):
+            nc.vector.tensor_tensor(m[u][:, 2 * b : 2 * b + 2, :], f_ps[u][b][:], g[u][:, 2 * b : 2 * b + 2, :], MULT)
+
+        times(0, 0)
+        cb, sb_ = quant("a1", a_g[1], V)
+        f_product(1, c3, s3, cb, sb_)
+        times(0, 1)
+        times(1, 0)
+        times(1, 1)
+        z_g = tile("z_g", [P, 4 * V], BF16)
+        nc.vector.tensor_tensor(
+            z_g[:].rearrange("p (c i t) -> p c t i", i=4, t=4),
+            m[0][:].rearrange("p t (c i) -> p c t i", i=4),
+            m[1][:].rearrange("p t (c i) -> p c t i", i=4),
+            ADD,
+        )
+        cz, sz = quant("z", z_g, V)
+        for b in range(2):
+            o_ps = ps.tile([P, S], F32, name="o_ps%d" % b, tag="h_ps%d" % b)
+            nc.tensor.matmul_mx(
+                out=o_ps[:, 0:V],
+                lhsT=w2w[:, 2 * b * P : 2 * (b + 1) * P].bitcast(FP4X4),
+                lhsT_scale=w2s[:, b * P : (b + 1) * P],
+                rhs=cz[:].bitcast(FP8X4),
+                rhs_scale=sz[:],
+                start=True,
+                stop=True,
+            )
+            o = tile("o%d" % b, [P, V], F32)
+            nc.scalar.activation(o[:], o_ps[:, 0:V], SILU)
+            nc.sync.dma_start(out[b * P : (b + 1) * P, :], o[:])

@@ -18,7 +18,8 @@ MULT = mybir.AluOpType.mult
 ADD = mybir.AluOpType.add
 
 P = 128
-W1_VECTOR_ROWS = 96
+W1_VECTOR_ROWS = 88
+W3_VECTOR_ROWS = 36
 
 
 def tile_picked_dime_silu_p_kernel(
@@ -27,32 +28,31 @@ def tile_picked_dime_silu_p_kernel(
     nc = tc.nc
     with ExitStack() as ctx:
         sb = ctx.enter_context(tc.tile_pool(name="sb", bufs=1))
+        stage = ctx.enter_context(tc.tile_pool(name="stage", bufs=1))
         ps = ctx.enter_context(tc.psum_pool(name="ps", bufs=1))
 
         def tile(name, shape, dtype):
             return sb.tile(shape, dtype, name=name, align_bytes=64)
 
+        def staged(name, shape, dtype, offset):
+            return stage.tile(shape, dtype, name=name, align_bytes=64, offset=offset)
+
         offs_t = tile("offs_t", [P, S // 16], U16)
         pos_t = [tile("pos1_t", [P, V // 16], U16), tile("pos2_t", [P, V // 16], U16)]
         xw = [tile("xw%d" % z, [P, T], I32) for z in range(2)]
         xs = tile("xs", [P, T], U8)
-        w1_raw = [tile("w1_raw%d" % z, [P, 4, H], F32) for z in range(2)]
-        w3_raw = [tile("w3_raw%d" % u, [P, 4, H // 2], F32) for u in range(2)]
-        a_raw = [tile("a_raw%d" % u, [P, 4, V], F32) for u in range(2)]
-        w2w = tile("w2w", [P, 2 * N], U8)
-        w2s = tile("w2s", [P, N], U8)
+        w1_raw = [staged("w1_raw%d" % z, [P, 4, H], F32, 8192 * z) for z in range(2)]
+        w3_raw = [staged("w3_raw%d" % u, [P, 4, H // 2], F32, 4096 + 4096 * u) for u in range(2)]
+        a_raw = [staged("a_raw%d" % u, [P, 4, V], F32, 12288 * u) for u in range(2)]
+        w2w = staged("w2w", [P, 2 * N], U8, 16384)
+        w2s = staged("w2s", [P, N], U8, 16384 + 512)
 
         warm = tile("warm", [P, 8], F32)
-        nc.gpsimd.memset(warm[:], 0.0)
+        nc.vector.memset(warm[:], 0.0)
         warm2 = tile("warm2", [P, 8], F32)
         nc.scalar.activation(warm2[:], warm[:], SILU)
 
-        nc.gpsimd.memset(xs[:].bitcast(I32), 0)
-        nc.gpsimd.memset(w2s[:].bitcast(I32), 0)
-        for q in range(4):
-            nc.gpsimd.dma_start(xs[32 * q : 32 * q + 8, :].bitcast(I32), x_scales[:, 4 * q : 4 * q + 4, :].bitcast(I32))
-        for q in range(4):
-            nc.gpsimd.dma_start(w2s[32 * q : 32 * q + 4, :].bitcast(I32), w2_scales[0, 4 * q : 4 * q + 4, :].bitcast(I32))
+        nc.vector.memset(xs[:].bitcast(I32), 0)
 
         def load_x(z):
             nc.sync.dma_start(xw[z][:], x_words[z].rearrange("p c r -> p (c r)").bitcast(I32))
@@ -62,16 +62,13 @@ def tile_picked_dime_silu_p_kernel(
 
         nc.sync.dma_start(w1_raw[0][:], rows4(w1[0:512, :]))
         nc.sync.dma_start(offs_t[:], offs)
-        load_x(0)
-        nc.sync.dma_start(w1_raw[1][:], rows4(w1[512:1024, :]))
-        load_x(1)
-        nc.sync.dma_start(w3_raw[0][:], rows4(w3[:, 0:256]))
         nc.sync.dma_start(pos_t[0][:], pos1)
         nc.sync.dma_start(pos_t[1][:], pos2)
-        nc.sync.dma_start(w3_raw[1][:], rows4(w3[:, 256:512]))
-        nc.sync.dma_start(a_raw[0][:], rows4(aT[:, 0:V]))
-        nc.sync.dma_start(a_raw[1][:], rows4(aT[:, V : 2 * V]))
-        nc.sync.dma_start(w2w[:], w2_words[0])
+        load_x(0)
+        for q in range(4):
+            nc.sync.dma_start(xs[32 * q : 32 * q + 8, :].bitcast(I32), x_scales[:, 4 * q : 4 * q + 4, :].bitcast(I32))
+        nc.sync.dma_start(w1_raw[1][:], rows4(w1[512:1024, :]))
+        load_x(1)
 
         def deal(engine_copy, grouped, raw, m0, m1, raw_m0):
             dst = grouped[:].rearrange("p (t m j) -> p m j t", t=4, j=4)[:, m0:m1]
@@ -84,107 +81,136 @@ def tile_picked_dime_silu_p_kernel(
             nc.vector.quantize_mx(out=codes[:].bitcast(FP8X4), scales=scales[:], in_=grouped[:])
             return codes, scales
 
-        w1_g = [tile("w1_g%d" % z, [P, 4 * H], BF16) for z in range(2)]
+        w1_g = [tile("w1_g0", [P, 4 * H], BF16), staged("w1_g1", [P, 4 * H], BF16, 16384)]
         w3_g = tile("w3_g", [P, 4 * H], BF16)
         a_g = [tile("a_g%d" % u, [P, 4 * V], BF16) for u in range(2)]
         xg = [tile("xg%d" % z, [P, S], U32) for z in range(2)]
         xsg = tile("xsg", [P, S], U8)
-        h_ps = [ps.tile([P, S], F32, name="h_ps%d" % t) for t in range(4)]
+        h_ps = [ps.tile([P, S], F32, name="h_ps%d" % t) for t in range(5)]
+        pieces = [(0, 0, 0, S // 2), (4, 0, S // 2, S), (1, 1, 0, S), (2, 2, 0, S), (3, 3, 0, S)]
 
-        def h_pass(z, codes, scales, t):
+        def h_pass(z, codes, scales, piece):
+            bank, t, c0, c1 = piece
             nc.tensor.matmul_mx(
-                out=h_ps[t][:],
+                out=h_ps[bank][:, c0:c1],
                 lhsT=codes[:, t * P : (t + 1) * P].bitcast(FP8X4),
                 lhsT_scale=scales[:, t * P : (t + 1) * P],
-                rhs=xg[z][:].bitcast(FP8X4),
-                rhs_scale=xsg[4 * z : P, :],
+                rhs=xg[z][:, c0:c1].bitcast(FP8X4),
+                rhs_scale=xsg[4 * z : P, c0:c1],
                 start=(z == 0),
                 stop=(z == 1),
             )
 
         deal(nc.scalar.copy, w1_g[0], w1_raw[0], 0, P, 0)
+        nc.sync.dma_start(a_raw[0][:], rows4(aT[:, 0:V]))
+        nc.sync.dma_start(w3_raw[0][:], rows4(w3[:, 0:256]))
         nc.vector.tensor_copy(xg[0][:], xw[0][:].bitcast(U32).indirect(offs_t[:]))
         c0, s0 = quant("w1a", w1_g[0], H)
         nc.vector.tensor_copy(xsg[:], xs[:].indirect(offs_t[:]))
-        for t in range(4):
-            h_pass(0, c0, s0, t)
+        for piece in pieces:
+            h_pass(0, c0, s0, piece)
         deal(nc.vector.tensor_copy, w1_g[1], w1_raw[1], 0, W1_VECTOR_ROWS, 0)
         deal(nc.scalar.copy, w1_g[1], w1_raw[1], W1_VECTOR_ROWS, P, 0)
+        nc.sync.dma_start(w3_raw[1][:], rows4(w3[:, 256:512]))
+        nc.sync.dma_start(a_raw[1][:], rows4(aT[:, V : 2 * V]))
         c1, s1 = quant("w1b", w1_g[1], H)
-        nc.vector.tensor_copy(xg[1][:], xw[1][:].bitcast(U32).indirect(offs_t[:]))
-        h = [tile("h%d" % t, [P, S], F32) for t in range(4)]
-        for t in range(4):
-            h_pass(1, c1, s1, t)
-            nc.scalar.activation(h[t][:], h_ps[t][:], SILU)
-        deal(nc.vector.tensor_copy, w3_g, w3_raw[0], 0, 64, 0)
-        deal(nc.scalar.copy, w3_g, w3_raw[1], 64, P, 64)
+        nc.sync.dma_start(w2w[:], w2_words[0])
+        for q in range(4):
+            nc.sync.dma_start(w2s[32 * q : 32 * q + 4, :].bitcast(I32), w2_scales[0, 4 * q : 4 * q + 4, :].bitcast(I32))
+        for u in range(2):
+            nc.vector.tensor_copy(xg[1][:, u * 256 : (u + 1) * 256], xw[1][:].bitcast(U32).indirect(offs_t[:, 16 * u : 16 * u + 16]))
+        h = [tile("h%d" % t, [P, S], F32) for t in range(2)] + [staged("h2", [P, S], F32, 4096), staged("h3", [P, S], F32, 12288)]
+        for piece in pieces:
+            h_pass(1, c1, s1, piece)
 
-        def weave(u):
+        def silu(piece):
+            bank, t, c0, c1 = piece
+            nc.scalar.activation(h[t][:, c0:c1], h_ps[bank][:, c0:c1], SILU)
+
+        def weave(engine_copy, u):
             dst = a_g[u][:].rearrange("p (c i j) -> p c j i", i=4, j=4)
             src = a_raw[u][:].rearrange("p j (c i) -> p c j i", i=4)
-            nc.scalar.copy(dst, src)
+            engine_copy(dst, src)
 
-        weave(0)
-        weave(1)
+        weave(nc.vector.tensor_copy, 0)
+        ca, sa = quant("a0", a_g[0], V)
+        silu(pieces[0])
+        silu(pieces[1])
+        silu(pieces[2])
+        deal(nc.scalar.copy, w3_g, w3_raw[0], 0, 64, 0)
+        silu(pieces[3])
+        deal(nc.scalar.copy, w3_g, w3_raw[1], 64, P - W3_VECTOR_ROWS, 64)
+        weave(nc.scalar.copy, 1)
+        silu(pieces[4])
 
         g = [tile("g%d" % u, [P, 4, V], F32) for u in range(2)]
 
         def fetch(u, t):
             nc.vector.tensor_copy(g[u][:, t, :], h[t][:].indirect(pos_t[u][:]))
 
-        f_ps = [[ps.tile([P, 2, V], F32, name="f_ps%d%d" % (u, b)) for b in range(2)] for u in range(2)]
+        f_ps = [[ps.tile([P, 4, P], F32, name="f_ps%d%d" % (u, b), tag="f_ps%d%d" % (u, b) if u + b < 2 else "h_ps0") for b in range(2)] for u in range(2)]
 
-        def f_product(u, wc, ws, ac, asc):
-            for t in range(4):
+        def f_product(u, ac, asc):
+            for b in range(2):
+                for t in range(4):
+                    nc.tensor.matmul_mx(
+                        out=f_ps[u][b][:, t, :],
+                        lhsT=c3[:, t * P : (t + 1) * P].bitcast(FP8X4),
+                        lhsT_scale=s3[:, t * P : (t + 1) * P],
+                        rhs=ac[:, b * P : (b + 1) * P].bitcast(FP8X4),
+                        rhs_scale=asc[:, b * P : (b + 1) * P],
+                        start=True,
+                        stop=True,
+                    )
+
+        for t in range(2):
+            fetch(0, t)
+            fetch(1, t)
+        deal(nc.vector.tensor_copy, w3_g, w3_raw[1], P - W3_VECTOR_ROWS, P, 64)
+        fetch(0, 2)
+        fetch(1, 2)
+        c3, s3 = quant("w3", w3_g, H)
+        f_product(0, ca, sa)
+        cb, sb_ = quant("a1", a_g[1], V)
+        f_product(1, cb, sb_)
+        fetch(0, 3)
+        fetch(1, 3)
+        m = [[tile("m%d%d" % (u, b), [P, 4, P], F32) for b in range(2)] for u in range(2)]
+        z_g = [tile("z_g%d" % b, [P, 4 * P], BF16) for b in range(2)]
+
+        def times(u, b):
+            nc.vector.tensor_tensor(m[u][b][:], f_ps[u][b][:], g[u][:, :, b * P : (b + 1) * P], MULT)
+
+        def join(b):
+            nc.vector.tensor_tensor(
+                z_g[b][:].rearrange("p (c i t) -> p c t i", i=4, t=4),
+                m[0][b][:].rearrange("p t (c i) -> p c t i", i=4),
+                m[1][b][:].rearrange("p t (c i) -> p c t i", i=4),
+                ADD,
+            )
+
+        def finish(b):
+            cz, sz = quant("z%d" % b, z_g[b], P)
+            o_ps = ps.tile([P, 4, P], F32, name="o_ps%d" % b, tag="h_ps%d" % (b + 1))
+            for r in range(2):
                 nc.tensor.matmul_mx(
-                    out=f_ps[u][t // 2][:, t % 2, :],
-                    lhsT=wc[:, t * P : (t + 1) * P].bitcast(FP8X4),
-                    lhsT_scale=ws[:, t * P : (t + 1) * P],
-                    rhs=ac[:].bitcast(FP8X4),
-                    rhs_scale=asc[:],
+                    out=o_ps[:, r, :],
+                    lhsT=w2w[:, 2 * r * P : 2 * (r + 1) * P].bitcast(FP4X4),
+                    lhsT_scale=w2s[:, r * P : (r + 1) * P],
+                    rhs=cz[:].bitcast(FP8X4),
+                    rhs_scale=sz[:],
                     start=True,
                     stop=True,
                 )
-
-        for t in range(4):
-            fetch(0, t)
-        fetch(1, 0)
-        c3, s3 = quant("w3", w3_g, H)
-        fetch(1, 1)
-        fetch(1, 2)
-        ca, sa = quant("a0", a_g[0], V)
-        f_product(0, c3, s3, ca, sa)
-        fetch(1, 3)
-        m = [tile("m%d" % u, [P, 4, V], F32) for u in range(2)]
-
-        def times(u, b):
-            nc.vector.tensor_tensor(m[u][:, 2 * b : 2 * b + 2, :], f_ps[u][b][:], g[u][:, 2 * b : 2 * b + 2, :], MULT)
+            o = tile("o%d" % b, [P, 2, P], F32)
+            nc.scalar.activation(o[:], o_ps[:, 0:2, :], SILU)
+            nc.scalar.dma_start(out[:, b * P : (b + 1) * P].rearrange("(r p) v -> p r v", p=P), o[:])
 
         times(0, 0)
-        cb, sb_ = quant("a1", a_g[1], V)
-        f_product(1, c3, s3, cb, sb_)
-        times(0, 1)
         times(1, 0)
+        times(0, 1)
+        join(0)
         times(1, 1)
-        z_g = tile("z_g", [P, 4 * V], BF16)
-        nc.vector.tensor_tensor(
-            z_g[:].rearrange("p (c i t) -> p c t i", i=4, t=4),
-            m[0][:].rearrange("p t (c i) -> p c t i", i=4),
-            m[1][:].rearrange("p t (c i) -> p c t i", i=4),
-            ADD,
-        )
-        cz, sz = quant("z", z_g, V)
-        for b in range(2):
-            o_ps = ps.tile([P, S], F32, name="o_ps%d" % b, tag="h_ps%d" % b)
-            nc.tensor.matmul_mx(
-                out=o_ps[:, 0:V],
-                lhsT=w2w[:, 2 * b * P : 2 * (b + 1) * P].bitcast(FP4X4),
-                lhsT_scale=w2s[:, b * P : (b + 1) * P],
-                rhs=cz[:].bitcast(FP8X4),
-                rhs_scale=sz[:],
-                start=True,
-                stop=True,
-            )
-            o = tile("o%d" % b, [P, V], F32)
-            nc.scalar.activation(o[:], o_ps[:, 0:V], SILU)
-            nc.sync.dma_start(out[b * P : (b + 1) * P, :], o[:])
+        finish(0)
+        join(1)
+        finish(1)

@@ -18,8 +18,8 @@ MULT = mybir.AluOpType.mult
 ADD = mybir.AluOpType.add
 
 P = 128
+W1A_VECTOR_ROWS = 64
 W1_VECTOR_ROWS = 88
-W3_VECTOR_ROWS = 36
 
 
 def tile_picked_dime_silu_p_kernel(
@@ -39,20 +39,20 @@ def tile_picked_dime_silu_p_kernel(
 
         offs_t = tile("offs_t", [P, S // 16], U16)
         pos_t = [tile("pos1_t", [P, V // 16], U16), tile("pos2_t", [P, V // 16], U16)]
-        xw = [tile("xw%d" % z, [P, T], I32) for z in range(2)]
+        xw = [tile("xw0", [P, T], I32), staged("xw1", [P, T], I32, 16384)]
         xs = tile("xs", [P, T], U8)
         w1_raw = [staged("w1_raw%d" % z, [P, 4, H], F32, 8192 * z) for z in range(2)]
         w3_raw = [staged("w3_raw%d" % u, [P, 4, H // 2], F32, 4096 + 4096 * u) for u in range(2)]
         a_raw = [staged("a_raw%d" % u, [P, 4, V], F32, 12288 * u) for u in range(2)]
-        w2w = staged("w2w", [P, 2 * N], U8, 16384)
-        w2s = staged("w2s", [P, N], U8, 16384 + 512)
-
-        warm = tile("warm", [P, 8], F32)
-        nc.vector.memset(warm[:], 0.0)
-        warm2 = tile("warm2", [P, 8], F32)
-        nc.scalar.activation(warm2[:], warm[:], SILU)
+        w2w = staged("w2w", [P, 2 * N], U8, 24576)
+        w2s = staged("w2s", [P, N], U8, 24576 + 512)
 
         nc.vector.memset(xs[:].bitcast(I32), 0)
+
+        warm = staged("warm", [P, 32], F32, 8192 - 64)
+        nc.vector.memset(warm[:], 0.0)
+        warm2 = staged("warm2", [P, 32], F32, 16384 - 64)
+        nc.scalar.activation(warm2[:], warm[:], SILU)
 
         def load_x(z):
             nc.sync.dma_start(xw[z][:], x_words[z].rearrange("p c r -> p (c r)").bitcast(I32))
@@ -60,13 +60,13 @@ def tile_picked_dime_silu_p_kernel(
         def rows4(w):
             return w.rearrange("(p j) c -> p j c", j=4)
 
-        nc.sync.dma_start(w1_raw[0][:], rows4(w1[0:512, :]))
         nc.sync.dma_start(offs_t[:], offs)
+        load_x(0)
         nc.sync.dma_start(pos_t[0][:], pos1)
         nc.sync.dma_start(pos_t[1][:], pos2)
-        load_x(0)
         for q in range(4):
             nc.sync.dma_start(xs[32 * q : 32 * q + 8, :].bitcast(I32), x_scales[:, 4 * q : 4 * q + 4, :].bitcast(I32))
+        nc.sync.dma_start(w1_raw[0][:], rows4(w1[0:512, :]))
         nc.sync.dma_start(w1_raw[1][:], rows4(w1[512:1024, :]))
         load_x(1)
 
@@ -81,7 +81,7 @@ def tile_picked_dime_silu_p_kernel(
             nc.vector.quantize_mx(out=codes[:].bitcast(FP8X4), scales=scales[:], in_=grouped[:])
             return codes, scales
 
-        w1_g = [tile("w1_g0", [P, 4 * H], BF16), staged("w1_g1", [P, 4 * H], BF16, 16384)]
+        w1_g = [tile("w1_g0", [P, 4 * H], BF16), staged("w1_g1", [P, 4 * H], BF16, 24576)]
         w3_g = tile("w3_g", [P, 4 * H], BF16)
         a_g = [tile("a_g%d" % u, [P, 4 * V], BF16) for u in range(2)]
         xg = [tile("xg%d" % z, [P, S], U32) for z in range(2)]
@@ -101,12 +101,13 @@ def tile_picked_dime_silu_p_kernel(
                 stop=(z == 1),
             )
 
-        deal(nc.scalar.copy, w1_g[0], w1_raw[0], 0, P, 0)
+        nc.vector.tensor_copy(xg[0][:], xw[0][:].bitcast(U32).indirect(offs_t[:]))
+        nc.vector.tensor_copy(xsg[:], xs[:].indirect(offs_t[:]))
+        deal(nc.vector.tensor_copy, w1_g[0], w1_raw[0], 0, W1A_VECTOR_ROWS, 0)
+        deal(nc.scalar.copy, w1_g[0], w1_raw[0], W1A_VECTOR_ROWS, P, 0)
         nc.sync.dma_start(a_raw[0][:], rows4(aT[:, 0:V]))
         nc.sync.dma_start(w3_raw[0][:], rows4(w3[:, 0:256]))
-        nc.vector.tensor_copy(xg[0][:], xw[0][:].bitcast(U32).indirect(offs_t[:]))
         c0, s0 = quant("w1a", w1_g[0], H)
-        nc.vector.tensor_copy(xsg[:], xs[:].indirect(offs_t[:]))
         for piece in pieces:
             h_pass(0, c0, s0, piece)
         deal(nc.vector.tensor_copy, w1_g[1], w1_raw[1], 0, W1_VECTOR_ROWS, 0)
@@ -133,13 +134,12 @@ def tile_picked_dime_silu_p_kernel(
             engine_copy(dst, src)
 
         weave(nc.vector.tensor_copy, 0)
-        ca, sa = quant("a0", a_g[0], V)
         silu(pieces[0])
         silu(pieces[1])
         silu(pieces[2])
         deal(nc.scalar.copy, w3_g, w3_raw[0], 0, 64, 0)
         silu(pieces[3])
-        deal(nc.scalar.copy, w3_g, w3_raw[1], 64, P - W3_VECTOR_ROWS, 64)
+        deal(nc.scalar.copy, w3_g, w3_raw[1], 64, P, 64)
         weave(nc.scalar.copy, 1)
         silu(pieces[4])
 
@@ -163,10 +163,11 @@ def tile_picked_dime_silu_p_kernel(
                         stop=True,
                     )
 
-        for t in range(2):
-            fetch(0, t)
-            fetch(1, t)
-        deal(nc.vector.tensor_copy, w3_g, w3_raw[1], P - W3_VECTOR_ROWS, P, 64)
+        fetch(0, 0)
+        ca, sa = quant("a0", a_g[0], V)
+        fetch(1, 0)
+        fetch(0, 1)
+        fetch(1, 1)
         fetch(0, 2)
         fetch(1, 2)
         c3, s3 = quant("w3", w3_g, H)

@@ -83,7 +83,7 @@ def tile_picked_dime_silu_p_kernel(
 
         w1_g = [tile("w1_g0", [P, 4 * H], BF16), staged("w1_g1", [P, 4 * H], BF16, 24576)]
         w3_g = tile("w3_g", [P, 4 * H], BF16)
-        a_g = [tile("a_g%d" % u, [P, 4 * V], BF16) for u in range(2)]
+        a_g = [tile("a_g0", [P, 4 * V], BF16), staged("a_g1", [P, 4 * V], BF16, 28672)]
         xg = [tile("xg%d" % z, [P, S], U32) for z in range(2)]
         xsg = tile("xsg", [P, S], U8)
         h_ps = [ps.tile([P, S], F32, name="h_ps%d" % t) for t in range(5)]
@@ -120,7 +120,7 @@ def tile_picked_dime_silu_p_kernel(
             nc.sync.dma_start(w2s[32 * q : 32 * q + 4, :].bitcast(I32), w2_scales[0, 4 * q : 4 * q + 4, :].bitcast(I32))
         for u in range(2):
             nc.vector.tensor_copy(xg[1][:, u * 256 : (u + 1) * 256], xw[1][:].bitcast(U32).indirect(offs_t[:, 16 * u : 16 * u + 16]))
-        h = [tile("h%d" % t, [P, S], F32) for t in range(2)] + [staged("h2", [P, S], F32, 4096), staged("h3", [P, S], F32, 12288)]
+        h = [tile("h%d" % t, [P, S], F32) for t in range(2)] + [staged("h2", [P, S], F32, 4096), staged("h3", [P, S], F32, 8192)]
         for piece in pieces:
             h_pass(1, c1, s1, piece)
 
@@ -140,8 +140,8 @@ def tile_picked_dime_silu_p_kernel(
         deal(nc.scalar.copy, w3_g, w3_raw[0], 0, 64, 0)
         silu(pieces[3])
         deal(nc.scalar.copy, w3_g, w3_raw[1], 64, P, 64)
-        weave(nc.scalar.copy, 1)
         silu(pieces[4])
+        weave(nc.scalar.copy, 1)
 
         g = [tile("g%d" % u, [P, 4, V], F32) for u in range(2)]
 
@@ -172,11 +172,12 @@ def tile_picked_dime_silu_p_kernel(
         fetch(1, 2)
         c3, s3 = quant("w3", w3_g, H)
         f_product(0, ca, sa)
-        cb, sb_ = quant("a1", a_g[1], V)
-        f_product(1, cb, sb_)
         fetch(0, 3)
         fetch(1, 3)
-        m = [[tile("m%d%d" % (u, b), [P, 4, P], F32) for b in range(2)] for u in range(2)]
+        m = [
+            [tile("m00", [P, 4, P], F32), staged("m01", [P, 4, P], F32, 28672)],
+            [tile("m10", [P, 4, P], F32), tile("m11", [P, 4, P], F32)],
+        ]
         z_g = [tile("z_g%d" % b, [P, 4 * P], BF16) for b in range(2)]
 
         def times(u, b):
@@ -192,10 +193,10 @@ def tile_picked_dime_silu_p_kernel(
 
         def finish(b):
             cz, sz = quant("z%d" % b, z_g[b], P)
-            o_ps = ps.tile([P, 4, P], F32, name="o_ps%d" % b, tag="h_ps%d" % (b + 1))
             for r in range(2):
+                o_ps = ps.tile([P, P], F32, name="o_ps%d%d" % (b, r), tag="h_ps%d" % (1 + 2 * b + r))
                 nc.tensor.matmul_mx(
-                    out=o_ps[:, r, :],
+                    out=o_ps[:],
                     lhsT=w2w[:, 2 * r * P : 2 * (r + 1) * P].bitcast(FP4X4),
                     lhsT_scale=w2s[:, r * P : (r + 1) * P],
                     rhs=cz[:].bitcast(FP8X4),
@@ -203,13 +204,15 @@ def tile_picked_dime_silu_p_kernel(
                     start=True,
                     stop=True,
                 )
-            o = tile("o%d" % b, [P, 2, P], F32)
-            nc.scalar.activation(o[:], o_ps[:, 0:2, :], SILU)
-            nc.scalar.dma_start(out[:, b * P : (b + 1) * P].rearrange("(r p) v -> p r v", p=P), o[:])
+                o = tile("o%d%d" % (b, r), [P, P], F32)
+                nc.scalar.activation(o[:], o_ps[:], SILU)
+                nc.sync.dma_start(out[r * P : (r + 1) * P, b * P : (b + 1) * P], o[:])
 
         times(0, 0)
-        times(1, 0)
+        cb, sb_ = quant("a1", a_g[1], V)
+        f_product(1, cb, sb_)
         times(0, 1)
+        times(1, 0)
         join(0)
         times(1, 1)
         finish(0)

@@ -40,18 +40,18 @@ def tile_picked_dime_silu_p_kernel(
         offs_t = tile("offs_t", [P, S // 16], U16)
         pos_t = [tile("pos1_t", [P, V // 16], U16), tile("pos2_t", [P, V // 16], U16)]
         xw = [tile("xw0", [P, T], I32), staged("xw1", [P, T], I32, 16384)]
-        xs = tile("xs", [P, T], U8)
+        xs = staged("xs", [P, T], U8, 23552)
         w1_raw = [staged("w1_raw%d" % z, [P, 4, H], F32, 8192 * z) for z in range(2)]
         w3_raw = [staged("w3_raw%d" % u, [P, 4, H // 2], F32, 4096 + 4096 * u) for u in range(2)]
         a_raw = [staged("a_raw%d" % u, [P, 4, V], F32, 12288 * u) for u in range(2)]
-        w2w = staged("w2w", [P, 2 * N], U8, 24576)
-        w2s = staged("w2s", [P, N], U8, 24576 + 512)
+        w2w = staged("w2w", [P, 2 * N], U8, 26624)
+        w2s = staged("w2s", [P, N], U8, 26624 + 512)
 
         nc.vector.memset(xs[:].bitcast(I32), 0)
 
         warm = staged("warm", [P, 32], F32, 8192 - 64)
         nc.vector.memset(warm[:], 0.0)
-        warm2 = staged("warm2", [P, 32], F32, 16384 - 64)
+        warm2 = tile("warm2", [P, 32], F32)
         nc.scalar.activation(warm2[:], warm[:], SILU)
 
         def load_x(z):
@@ -64,11 +64,9 @@ def tile_picked_dime_silu_p_kernel(
         load_x(0)
         nc.sync.dma_start(pos_t[0][:], pos1)
         nc.sync.dma_start(pos_t[1][:], pos2)
-        for q in range(4):
-            nc.sync.dma_start(xs[32 * q : 32 * q + 8, :].bitcast(I32), x_scales[:, 4 * q : 4 * q + 4, :].bitcast(I32))
+        nc.sync.dma_start(xs[0:P:4, :].bitcast(I32), x_scales.rearrange("z q c -> (z q) c").bitcast(I32))
         nc.sync.dma_start(w1_raw[0][:], rows4(w1[0:512, :]))
         nc.sync.dma_start(w1_raw[1][:], rows4(w1[512:1024, :]))
-        load_x(1)
 
         def deal(engine_copy, grouped, raw, m0, m1, raw_m0):
             dst = grouped[:].rearrange("p (t m j) -> p m j t", t=4, j=4)[:, m0:m1]
@@ -81,11 +79,12 @@ def tile_picked_dime_silu_p_kernel(
             nc.vector.quantize_mx(out=codes[:].bitcast(FP8X4), scales=scales[:], in_=grouped[:])
             return codes, scales
 
-        w1_g = [tile("w1_g0", [P, 4 * H], BF16), staged("w1_g1", [P, 4 * H], BF16, 24576)]
+        w1_g = [tile("w1_g0", [P, 4 * H], BF16), staged("w1_g1", [P, 4 * H], BF16, 26624)]
         w3_g = tile("w3_g", [P, 4 * H], BF16)
-        a_g = [tile("a_g0", [P, 4 * V], BF16), staged("a_g1", [P, 4 * V], BF16, 28672)]
-        xg = [tile("xg%d" % z, [P, S], U32) for z in range(2)]
-        xsg = tile("xsg", [P, S], U8)
+        a_g = [staged("a_g0", [P, 4 * V], BF16, 32768), staged("a_g1", [P, 4 * V], BF16, 10240)]
+        xg = [staged("xg0", [P, S], U32, 24576), tile("xg1", [P, S], U32)]
+        xs_rows = tile("xs_rows", [P, S], U8)
+        xsg = [tile("xsg%d" % z, [P, S], U8) for z in range(2)]
         h_ps = [ps.tile([P, S], F32, name="h_ps%d" % t) for t in range(5)]
         pieces = [(0, 0, 0, S // 2), (4, 0, S // 2, S), (1, 1, 0, S), (2, 2, 0, S), (3, 3, 0, S)]
 
@@ -96,13 +95,24 @@ def tile_picked_dime_silu_p_kernel(
                 lhsT=codes[:, t * P : (t + 1) * P].bitcast(FP8X4),
                 lhsT_scale=scales[:, t * P : (t + 1) * P],
                 rhs=xg[z][:, c0:c1].bitcast(FP8X4),
-                rhs_scale=xsg[4 * z : P, c0:c1],
+                rhs_scale=xsg[z][:, c0:c1],
                 start=(z == 0),
                 stop=(z == 1),
             )
 
+        def place_scales(z):
+            for q in range(4):
+                row = 16 * z + 4 * q
+                nc.sync.dma_start(
+                    xsg[z][32 * q : 32 * q + 4, :].bitcast(I32),
+                    xs_rows[4 * row : 4 * row + 16 : 4, :].bitcast(I32),
+                )
+
+        nc.vector.tensor_copy(xs_rows[:], xs[:].indirect(offs_t[:]))
+        place_scales(0)
+        load_x(1)
+        place_scales(1)
         nc.vector.tensor_copy(xg[0][:], xw[0][:].bitcast(U32).indirect(offs_t[:]))
-        nc.vector.tensor_copy(xsg[:], xs[:].indirect(offs_t[:]))
         deal(nc.vector.tensor_copy, w1_g[0], w1_raw[0], 0, W1A_VECTOR_ROWS, 0)
         deal(nc.scalar.copy, w1_g[0], w1_raw[0], W1A_VECTOR_ROWS, P, 0)
         nc.sync.dma_start(a_raw[0][:], rows4(aT[:, 0:V]))
@@ -120,7 +130,7 @@ def tile_picked_dime_silu_p_kernel(
             nc.sync.dma_start(w2s[32 * q : 32 * q + 4, :].bitcast(I32), w2_scales[0, 4 * q : 4 * q + 4, :].bitcast(I32))
         for u in range(2):
             nc.vector.tensor_copy(xg[1][:, u * 256 : (u + 1) * 256], xw[1][:].bitcast(U32).indirect(offs_t[:, 16 * u : 16 * u + 16]))
-        h = [tile("h%d" % t, [P, S], F32) for t in range(2)] + [staged("h2", [P, S], F32, 4096), staged("h3", [P, S], F32, 8192)]
+        h = [tile("h%d" % t, [P, S], F32) for t in range(3)] + [staged("h3", [P, S], F32, 8192)]
         for piece in pieces:
             h_pass(1, c1, s1, piece)
 
@@ -137,13 +147,13 @@ def tile_picked_dime_silu_p_kernel(
         silu(pieces[0])
         silu(pieces[1])
         silu(pieces[2])
-        deal(nc.scalar.copy, w3_g, w3_raw[0], 0, 64, 0)
         silu(pieces[3])
+        deal(nc.scalar.copy, w3_g, w3_raw[0], 0, 64, 0)
         deal(nc.scalar.copy, w3_g, w3_raw[1], 64, P, 64)
         silu(pieces[4])
         weave(nc.scalar.copy, 1)
 
-        g = [tile("g%d" % u, [P, 4, V], F32) for u in range(2)]
+        g = [staged("g0", [P, 4, V], F32, 0), staged("g1", [P, 4, V], F32, 32768)]
 
         def fetch(u, t):
             nc.vector.tensor_copy(g[u][:, t, :], h[t][:].indirect(pos_t[u][:]))
@@ -163,8 +173,8 @@ def tile_picked_dime_silu_p_kernel(
                         stop=True,
                     )
 
-        fetch(0, 0)
         ca, sa = quant("a0", a_g[0], V)
+        fetch(0, 0)
         fetch(1, 0)
         fetch(0, 1)
         fetch(1, 1)
@@ -175,7 +185,7 @@ def tile_picked_dime_silu_p_kernel(
         fetch(0, 3)
         fetch(1, 3)
         m = [
-            [tile("m00", [P, 4, P], F32), staged("m01", [P, 4, P], F32, 28672)],
+            [tile("m00", [P, 4, P], F32), staged("m01", [P, 4, P], F32, 10240)],
             [tile("m10", [P, 4, P], F32), tile("m11", [P, 4, P], F32)],
         ]
         z_g = [tile("z_g%d" % b, [P, 4 * P], BF16) for b in range(2)]

@@ -19,7 +19,8 @@ ADD = mybir.AluOpType.add
 
 P = 128
 W1A_VECTOR_ROWS = 64
-W1_VECTOR_ROWS = 88
+W3_VECTOR_ROWS = 88
+W1B_VECTOR_ROWS = 88
 
 
 def tile_picked_dime_silu_p_kernel(
@@ -39,17 +40,17 @@ def tile_picked_dime_silu_p_kernel(
 
         offs_t = tile("offs_t", [P, S // 16], U16)
         pos_t = [tile("pos1_t", [P, V // 16], U16), tile("pos2_t", [P, V // 16], U16)]
-        xw = [tile("xw0", [P, T], I32), staged("xw1", [P, T], I32, 16384)]
-        xs = staged("xs", [P, T], U8, 23552)
-        w1_raw = [staged("w1_raw%d" % z, [P, 4, H], F32, 8192 * z) for z in range(2)]
-        w3_raw = [staged("w3_raw%d" % u, [P, 4, H // 2], F32, 4096 + 4096 * u) for u in range(2)]
-        a_raw = [staged("a_raw%d" % u, [P, 4, V], F32, 12288 * u) for u in range(2)]
-        w2w = staged("w2w", [P, 2 * N], U8, 26624)
-        w2s = staged("w2s", [P, N], U8, 26624 + 512)
+        w1_raw = [staged("w1_raw0", [P, 4, H], F32, 8192), staged("w1_raw1", [P, 4, H], F32, 31232)]
+        w3_raw = staged("w3_raw", [P, 4, H], F32, 16384)
+        xs = staged("xs", [P, T], U8, 51200)
+        xw = [staged("xw0", [P, T], I32, 40960), staged("xw1", [P, T], I32, 512)]
+        a_raw = [staged("a_raw0", [P, 4, V], F32, 25088), staged("a_raw1", [P, 4, V], F32, 16384)]
+        w2w = staged("w2w", [P, 2 * N], U8, 25088)
+        w2s = staged("w2s", [P, N], U8, 25600)
 
-        nc.vector.memset(xs[:].bitcast(I32), 0)
+        nc.vector.memset(xs[:, :].bitcast(I32), 0)
 
-        warm = staged("warm", [P, 32], F32, 8192 - 64)
+        warm = tile("warm", [P, 32], F32)
         nc.vector.memset(warm[:], 0.0)
         warm2 = tile("warm2", [P, 32], F32)
         nc.scalar.activation(warm2[:], warm[:], SILU)
@@ -60,17 +61,14 @@ def tile_picked_dime_silu_p_kernel(
         def rows4(w):
             return w.rearrange("(p j) c -> p j c", j=4)
 
-        nc.sync.dma_start(offs_t[:], offs)
-        load_x(0)
-        nc.sync.dma_start(pos_t[0][:], pos1)
-        nc.sync.dma_start(pos_t[1][:], pos2)
-        nc.sync.dma_start(xs[0:P:4, :].bitcast(I32), x_scales.rearrange("z q c -> (z q) c").bitcast(I32))
-        nc.sync.dma_start(w1_raw[0][:], rows4(w1[0:512, :]))
-        nc.sync.dma_start(w1_raw[1][:], rows4(w1[512:1024, :]))
-
-        def deal(engine_copy, grouped, raw, m0, m1, raw_m0):
+        def deal(engine_copy, grouped, raw, m0, m1):
             dst = grouped[:].rearrange("p (t m j) -> p m j t", t=4, j=4)[:, m0:m1]
-            src = raw[:].rearrange("p j (m t) -> p m j t", t=4)[:, m0 - raw_m0 : m1 - raw_m0]
+            src = raw[:].rearrange("p j (m t) -> p m j t", t=4)[:, m0:m1]
+            engine_copy(dst, src)
+
+        def weave(engine_copy, u, c0, c1):
+            dst = a_g[u][:].rearrange("p (c i j) -> p c j i", i=4, j=4)[:, c0:c1]
+            src = a_raw[u][:].rearrange("p j (c i) -> p c j i", i=4)[:, c0:c1]
             engine_copy(dst, src)
 
         def quant(name, grouped, width):
@@ -79,14 +77,18 @@ def tile_picked_dime_silu_p_kernel(
             nc.vector.quantize_mx(out=codes[:].bitcast(FP8X4), scales=scales[:], in_=grouped[:])
             return codes, scales
 
-        w1_g = [tile("w1_g0", [P, 4 * H], BF16), staged("w1_g1", [P, 4 * H], BF16, 26624)]
+        w1_g = [tile("w1_g%d" % z, [P, 4 * H], BF16) for z in range(2)]
         w3_g = tile("w3_g", [P, 4 * H], BF16)
-        a_g = [staged("a_g0", [P, 4 * V], BF16, 32768), staged("a_g1", [P, 4 * V], BF16, 10240)]
-        xg = [staged("xg0", [P, S], U32, 24576), tile("xg1", [P, S], U32)]
+        a_g = [tile("a_g%d" % u, [P, 4 * V], BF16) for u in range(2)]
+        xg = [tile("xg0", [P, S], U32), tile("xg1", [P, S], U32)]
         xs_rows = tile("xs_rows", [P, S], U8)
-        xsg = [tile("xsg%d" % z, [P, S], U8) for z in range(2)]
+        xsg = [tile("xsg0", [P, S], U8), staged("xsg1", [P, S], U8, 8704)]
         h_ps = [ps.tile([P, S], F32, name="h_ps%d" % t) for t in range(5)]
         pieces = [(0, 0, 0, S // 2), (4, 0, S // 2, S), (1, 1, 0, S), (2, 2, 0, S), (3, 3, 0, S)]
+        h = [tile("h%d" % t, [P, S], F32) for t in range(4)]
+        f = [staged("f0", [P, 4, V], F32, 31232), tile("f1", [P, 4, V], F32)]
+        m = [staged("m0", [P, 4, V], F32, 16384), tile("m1", [P, 4, V], F32)]
+        z_g = [tile("z_g%d" % b, [P, 4 * P], BF16) for b in range(2)]
 
         def h_pass(z, codes, scales, piece):
             bank, t, c0, c1 = piece
@@ -108,96 +110,36 @@ def tile_picked_dime_silu_p_kernel(
                     xs_rows[4 * row : 4 * row + 16 : 4, :].bitcast(I32),
                 )
 
-        nc.vector.tensor_copy(xs_rows[:], xs[:].indirect(offs_t[:]))
-        place_scales(0)
-        load_x(1)
-        place_scales(1)
-        nc.vector.tensor_copy(xg[0][:], xw[0][:].bitcast(U32).indirect(offs_t[:]))
-        deal(nc.vector.tensor_copy, w1_g[0], w1_raw[0], 0, W1A_VECTOR_ROWS, 0)
-        deal(nc.scalar.copy, w1_g[0], w1_raw[0], W1A_VECTOR_ROWS, P, 0)
-        nc.sync.dma_start(a_raw[0][:], rows4(aT[:, 0:V]))
-        nc.sync.dma_start(w3_raw[0][:], rows4(w3[:, 0:256]))
-        c0, s0 = quant("w1a", w1_g[0], H)
-        for piece in pieces:
-            h_pass(0, c0, s0, piece)
-        deal(nc.vector.tensor_copy, w1_g[1], w1_raw[1], 0, W1_VECTOR_ROWS, 0)
-        deal(nc.scalar.copy, w1_g[1], w1_raw[1], W1_VECTOR_ROWS, P, 0)
-        nc.sync.dma_start(w3_raw[1][:], rows4(w3[:, 256:512]))
-        nc.sync.dma_start(a_raw[1][:], rows4(aT[:, V : 2 * V]))
-        c1, s1 = quant("w1b", w1_g[1], H)
-        nc.sync.dma_start(w2w[:], w2_words[0])
-        for q in range(4):
-            nc.sync.dma_start(w2s[32 * q : 32 * q + 4, :].bitcast(I32), w2_scales[0, 4 * q : 4 * q + 4, :].bitcast(I32))
-        for u in range(2):
-            nc.vector.tensor_copy(xg[1][:, u * 256 : (u + 1) * 256], xw[1][:].bitcast(U32).indirect(offs_t[:, 16 * u : 16 * u + 16]))
-        h = [tile("h%d" % t, [P, S], F32) for t in range(3)] + [staged("h3", [P, S], F32, 8192)]
-        for piece in pieces:
-            h_pass(1, c1, s1, piece)
+        def f_product(u, ac, asc):
+            for pair in range(2):
+                f_ps = ps.tile([P, 2, V], F32, name="f_ps%d%d" % (u, pair), tag="f_ps%d" % pair)
+                for e in range(2):
+                    t = 2 * pair + e
+                    nc.tensor.matmul_mx(
+                        out=f_ps[:, e, :],
+                        lhsT=c3[:, t * P : (t + 1) * P].bitcast(FP8X4),
+                        lhsT_scale=s3[:, t * P : (t + 1) * P],
+                        rhs=ac[:].bitcast(FP8X4),
+                        rhs_scale=asc[:],
+                        start=True,
+                        stop=True,
+                    )
+                nc.scalar.copy(f[u][:, 2 * pair : 2 * pair + 2, :], f_ps[:])
 
         def silu(piece):
             bank, t, c0, c1 = piece
             nc.scalar.activation(h[t][:, c0:c1], h_ps[bank][:, c0:c1], SILU)
 
-        def weave(engine_copy, u):
-            dst = a_g[u][:].rearrange("p (c i j) -> p c j i", i=4, j=4)
-            src = a_raw[u][:].rearrange("p j (c i) -> p c j i", i=4)
-            engine_copy(dst, src)
-
-        weave(nc.vector.tensor_copy, 0)
-        silu(pieces[0])
-        silu(pieces[1])
-        silu(pieces[2])
-        silu(pieces[3])
-        deal(nc.scalar.copy, w3_g, w3_raw[0], 0, 64, 0)
-        deal(nc.scalar.copy, w3_g, w3_raw[1], 64, P, 64)
-        silu(pieces[4])
-        weave(nc.scalar.copy, 1)
-
-        g = [staged("g0", [P, 4, V], F32, 0), staged("g1", [P, 4, V], F32, 32768)]
-
-        def fetch(u, t):
-            nc.vector.tensor_copy(g[u][:, t, :], h[t][:].indirect(pos_t[u][:]))
-
-        f_ps = [[ps.tile([P, 4, P], F32, name="f_ps%d%d" % (u, b), tag="f_ps%d%d" % (u, b) if u + b < 2 else "h_ps0") for b in range(2)] for u in range(2)]
-
-        def f_product(u, ac, asc):
-            for b in range(2):
-                for t in range(4):
-                    nc.tensor.matmul_mx(
-                        out=f_ps[u][b][:, t, :],
-                        lhsT=c3[:, t * P : (t + 1) * P].bitcast(FP8X4),
-                        lhsT_scale=s3[:, t * P : (t + 1) * P],
-                        rhs=ac[:, b * P : (b + 1) * P].bitcast(FP8X4),
-                        rhs_scale=asc[:, b * P : (b + 1) * P],
-                        start=True,
-                        stop=True,
-                    )
-
-        ca, sa = quant("a0", a_g[0], V)
-        fetch(0, 0)
-        fetch(1, 0)
-        fetch(0, 1)
-        fetch(1, 1)
-        fetch(0, 2)
-        fetch(1, 2)
-        c3, s3 = quant("w3", w3_g, H)
-        f_product(0, ca, sa)
-        fetch(0, 3)
-        fetch(1, 3)
-        m = [
-            [tile("m00", [P, 4, P], F32), staged("m01", [P, 4, P], F32, 10240)],
-            [tile("m10", [P, 4, P], F32), tile("m11", [P, 4, P], F32)],
-        ]
-        z_g = [tile("z_g%d" % b, [P, 4 * P], BF16) for b in range(2)]
-
-        def times(u, b):
-            nc.vector.tensor_tensor(m[u][b][:], f_ps[u][b][:], g[u][:, :, b * P : (b + 1) * P], MULT)
+        def fetch(u, t, v0, v1):
+            nc.vector.tensor_tensor(
+                m[u][:, t, v0:v1], h[t][:].indirect(pos_t[u][:, v0 // 16 : v1 // 16]), f[u][:, t, v0:v1], MULT
+            )
 
         def join(b):
             nc.vector.tensor_tensor(
                 z_g[b][:].rearrange("p (c i t) -> p c t i", i=4, t=4),
-                m[0][b][:].rearrange("p t (c i) -> p c t i", i=4),
-                m[1][b][:].rearrange("p t (c i) -> p c t i", i=4),
+                m[0][:, :, b * P : (b + 1) * P].rearrange("p t (c i) -> p c t i", i=4),
+                m[1][:, :, b * P : (b + 1) * P].rearrange("p t (c i) -> p c t i", i=4),
                 ADD,
             )
 
@@ -218,13 +160,56 @@ def tile_picked_dime_silu_p_kernel(
                 nc.scalar.activation(o[:], o_ps[:], SILU)
                 nc.sync.dma_start(out[r * P : (r + 1) * P, b * P : (b + 1) * P], o[:])
 
-        times(0, 0)
+        nc.sync.dma_start(offs_t[:], offs)
+        load_x(0)
+        nc.sync.dma_start(pos_t[0][:], pos1)
+        nc.sync.dma_start(pos_t[1][:], pos2)
+        nc.sync.dma_start(xs[0:P:4, :].bitcast(I32), x_scales.rearrange("z q c -> (z q) c").bitcast(I32))
+        nc.sync.dma_start(w1_raw[0][:], rows4(w1[0:512, :]))
+        nc.sync.dma_start(w3_raw[:], rows4(w3))
+
+        nc.sync.dma_start(a_raw[0][:], rows4(aT[:, 0:V]))
+        nc.sync.dma_start(w1_raw[1][:], rows4(w1[512:1024, :]))
+        nc.vector.tensor_copy(xs_rows[:], xs[:].indirect(offs_t[:]))
+        place_scales(0)
+        nc.vector.tensor_copy(xg[0][:], xw[0][:].bitcast(U32).indirect(offs_t[:]))
+
+        deal(nc.vector.tensor_copy, w1_g[0], w1_raw[0], 0, W1A_VECTOR_ROWS)
+        deal(nc.scalar.copy, w1_g[0], w1_raw[0], W1A_VECTOR_ROWS, P)
+        load_x(1)
+        place_scales(1)
+        c0, s0 = quant("w1a", w1_g[0], H)
+        for piece in pieces:
+            h_pass(0, c0, s0, piece)
+        deal(nc.vector.tensor_copy, w3_g, w3_raw, 0, W3_VECTOR_ROWS)
+        deal(nc.scalar.copy, w3_g, w3_raw, W3_VECTOR_ROWS, P)
+        nc.sync.dma_start(a_raw[1][:], rows4(aT[:, V : 2 * V]))
+        c3, s3 = quant("w3", w3_g, H)
+        weave(nc.scalar.copy, 0, 0, V // 4)
+        nc.sync.dma_start(w2w[:], w2_words[0])
+        for q in range(4):
+            nc.sync.dma_start(w2s[32 * q : 32 * q + 4, :].bitcast(I32), w2_scales[0, 4 * q : 4 * q + 4, :].bitcast(I32))
+        ca, sa = quant("a0", a_g[0], V)
+        deal(nc.vector.tensor_copy, w1_g[1], w1_raw[1], 0, W1B_VECTOR_ROWS)
+        deal(nc.scalar.copy, w1_g[1], w1_raw[1], W1B_VECTOR_ROWS, P)
+        f_product(0, ca, sa)
+        c1, s1 = quant("w1b", w1_g[1], H)
+        for u in range(2):
+            nc.vector.tensor_copy(xg[1][:, u * 256 : (u + 1) * 256], xw[1][:].bitcast(U32).indirect(offs_t[:, 16 * u : 16 * u + 16]))
+        for piece in pieces:
+            h_pass(1, c1, s1, piece)
+        weave(nc.vector.tensor_copy, 1, 0, V // 4)
+        for piece in pieces:
+            silu(piece)
         cb, sb_ = quant("a1", a_g[1], V)
         f_product(1, cb, sb_)
-        times(0, 1)
-        times(1, 0)
+        for t in range(4):
+            fetch(0, t, 0, V)
+        for t in range(3):
+            fetch(1, t, 0, V)
+        fetch(1, 3, 0, P)
+        fetch(1, 3, P, V)
         join(0)
-        times(1, 1)
         finish(0)
         join(1)
         finish(1)

@@ -1,6 +1,7 @@
 from contextlib import ExitStack
 
 import concourse.mybir as mybir
+from concourse.masks import make_identity
 
 K, T, S, V, H, N, J = 1024, 2048, 512, 256, 512, 256, 512
 FLOPS = 2 * K * H * S + 2 * J * H * 2 * V + 2 * H * N * V
@@ -55,6 +56,9 @@ def tile_picked_dime_silu_p_kernel(
         warm2 = tile("warm2", [P, 32], F32)
         nc.scalar.activation(warm2[:], warm[:], SILU)
 
+        ident = tile("ident", [P, P], F32)
+        make_identity(nc, ident[:])
+
         def load_x(z):
             nc.sync.dma_start(xw[z][:], x_words[z].rearrange("p c r -> p (c r)").bitcast(I32))
 
@@ -71,9 +75,9 @@ def tile_picked_dime_silu_p_kernel(
             src = a_raw[u][:].rearrange("p j (c i) -> p c j i", i=4)[:, c0:c1]
             engine_copy(dst, src)
 
-        def quant(name, grouped, width):
-            codes = tile(name + "_c", [P, width], U32)
-            scales = tile(name + "_s", [P, width], U8)
+        def quant(name, grouped, width, at=None):
+            codes = tile(name + "_c", [P, width], U32) if at is None else staged(name + "_c", [P, width], U32, at)
+            scales = tile(name + "_s", [P, width], U8) if at is None else staged(name + "_s", [P, width], U8, at + 4096)
             nc.vector.quantize_mx(out=codes[:].bitcast(FP8X4), scales=scales[:], in_=grouped[:])
             return codes, scales
 
@@ -85,8 +89,10 @@ def tile_picked_dime_silu_p_kernel(
         xsg = [tile("xsg0", [P, S], U8), staged("xsg1", [P, S], U8, 8704)]
         h_ps = [ps.tile([P, S], F32, name="h_ps%d" % t) for t in range(5)]
         pieces = [(0, 0, 0, S // 2), (4, 0, S // 2, S), (1, 1, 0, S), (2, 2, 0, S), (3, 3, 0, S)]
-        h = [tile("h%d" % t, [P, S], F32) for t in range(4)]
-        f = [staged("f0", [P, 4, V], F32, 31232), tile("f1", [P, 4, V], F32)]
+        h = [tile("h0", [P, S], F32), tile("h1", [P, S], F32), tile("h2", [P, S], F32), staged("h3", [P, S], F32, 59392 + 1024 - 64)]
+        f0_low = staged("f0_low", [P, 3, V], F32, 31232)
+        f0_high = [staged("f0_high0", [P, P], F32, 34304), staged("f0_high1", [P, P], F32, 63488)]
+        f1 = [tile("f1_%d" % b, [P, 4, P], F32) for b in range(2)]
         m = [staged("m0", [P, 4, V], F32, 16384), tile("m1", [P, 4, V], F32)]
         z_g = [tile("z_g%d" % b, [P, 4 * P], BF16) for b in range(2)]
 
@@ -110,30 +116,23 @@ def tile_picked_dime_silu_p_kernel(
                     xs_rows[4 * row : 4 * row + 16 : 4, :].bitcast(I32),
                 )
 
-        def f_product(u, ac, asc):
-            for pair in range(2):
-                f_ps = ps.tile([P, 2, V], F32, name="f_ps%d%d" % (u, pair), tag="f_ps%d" % pair)
-                for e in range(2):
-                    t = 2 * pair + e
-                    nc.tensor.matmul_mx(
-                        out=f_ps[:, e, :],
-                        lhsT=c3[:, t * P : (t + 1) * P].bitcast(FP8X4),
-                        lhsT_scale=s3[:, t * P : (t + 1) * P],
-                        rhs=ac[:].bitcast(FP8X4),
-                        rhs_scale=asc[:],
-                        start=True,
-                        stop=True,
-                    )
-                nc.scalar.copy(f[u][:, 2 * pair : 2 * pair + 2, :], f_ps[:])
+        def f_matmul(dst, t, ac, asc, v0, v1):
+            nc.tensor.matmul_mx(
+                out=dst,
+                lhsT=c3[:, t * P : (t + 1) * P].bitcast(FP8X4),
+                lhsT_scale=s3[:, t * P : (t + 1) * P],
+                rhs=ac[:, v0:v1].bitcast(FP8X4),
+                rhs_scale=asc[:, v0:v1],
+                start=True,
+                stop=True,
+            )
 
         def silu(piece):
             bank, t, c0, c1 = piece
             nc.scalar.activation(h[t][:, c0:c1], h_ps[bank][:, c0:c1], SILU)
 
-        def fetch(u, t, v0, v1):
-            nc.vector.tensor_tensor(
-                m[u][:, t, v0:v1], h[t][:].indirect(pos_t[u][:, v0 // 16 : v1 // 16]), f[u][:, t, v0:v1], MULT
-            )
+        def fetch(u, t, v0, v1, factor):
+            nc.vector.tensor_tensor(m[u][:, t, v0:v1], h[t][:].indirect(pos_t[u][:, v0 // 16 : v1 // 16]), factor, MULT)
 
         def join(b):
             nc.vector.tensor_tensor(
@@ -143,10 +142,25 @@ def tile_picked_dime_silu_p_kernel(
                 ADD,
             )
 
+        z_turned = tile("z_turned", [P, 2, 2 * P], BF16)
+        words_ps = []
+
+        def turned_sum(pair):
+            sum_ps = ps.tile([P, 2, P], F32, name="sum_ps%d" % pair, tag="h_ps%d" % pair)
+            for e in range(2):
+                for u in range(2):
+                    nc.tensor.matmul(
+                        sum_ps[:, e, :], m[u][:, 2 * pair + e, 0:P], ident[:], start=(u == 0), stop=(u == 1), is_transpose=True
+                    )
+            nc.scalar.copy(z_turned[:, pair, :].rearrange("v (p e) -> v p e", e=2), sum_ps[:].rearrange("v e p -> v p e"))
+            if pair == 0:
+                words_ps.append(ps.tile([P, 2, P], F32, name="words_ps", tag="h_ps2"))
+            nc.tensor.transpose(words_ps[0][:, pair, :], z_turned[:, pair, :].bitcast(F32), ident[:])
+
         def finish(b):
             cz, sz = quant("z%d" % b, z_g[b], P)
             for r in range(2):
-                o_ps = ps.tile([P, P], F32, name="o_ps%d%d" % (b, r), tag="h_ps%d" % (1 + 2 * b + r))
+                o_ps = ps.tile([P, P], F32, name="o_ps%d%d" % (b, r), tag=["h_ps3", "h_ps4", "f_ps0", "f_ps1"][2 * b + r])
                 nc.tensor.matmul_mx(
                     out=o_ps[:],
                     lhsT=w2w[:, 2 * r * P : 2 * (r + 1) * P].bitcast(FP4X4),
@@ -160,8 +174,8 @@ def tile_picked_dime_silu_p_kernel(
                 nc.scalar.activation(o[:], o_ps[:], SILU)
                 nc.sync.dma_start(out[r * P : (r + 1) * P, b * P : (b + 1) * P], o[:])
 
-        nc.sync.dma_start(offs_t[:], offs)
         load_x(0)
+        nc.sync.dma_start(offs_t[:], offs)
         nc.sync.dma_start(pos_t[0][:], pos1)
         nc.sync.dma_start(pos_t[1][:], pos2)
         nc.sync.dma_start(xs[0:P:4, :].bitcast(I32), x_scales.rearrange("z q c -> (z q) c").bitcast(I32))
@@ -192,24 +206,45 @@ def tile_picked_dime_silu_p_kernel(
         ca, sa = quant("a0", a_g[0], V)
         deal(nc.vector.tensor_copy, w1_g[1], w1_raw[1], 0, W1B_VECTOR_ROWS)
         deal(nc.scalar.copy, w1_g[1], w1_raw[1], W1B_VECTOR_ROWS, P)
-        f_product(0, ca, sa)
+        f0_ps = [ps.tile([P, 2, V], F32, name="f0_ps%d" % pair, tag="f_ps%d" % pair) for pair in range(2)]
+        for t in range(4):
+            f_matmul(f0_ps[t // 2][:, t % 2, :], t, ca, sa, 0, V)
+        nc.scalar.copy(f0_low[:, 0:2, :], f0_ps[0][:])
+        nc.scalar.copy(f0_low[:, 2, :], f0_ps[1][:, 0, :])
+        nc.scalar.copy(f0_high[0][:], f0_ps[1][:, 1, 0:P])
         c1, s1 = quant("w1b", w1_g[1], H)
         for u in range(2):
             nc.vector.tensor_copy(xg[1][:, u * 256 : (u + 1) * 256], xw[1][:].bitcast(U32).indirect(offs_t[:, 16 * u : 16 * u + 16]))
         for piece in pieces:
             h_pass(1, c1, s1, piece)
         weave(nc.vector.tensor_copy, 1, 0, V // 4)
-        for piece in pieces:
+        cb, sb_ = quant("a1", a_g[1], V, 59392)
+        f1_ps = [ps.tile([P, 4, P], F32, name="f1_ps%d" % b, tag=["f_ps0", "f_ps2"][b]) for b in range(2)]
+        for b in range(2):
+            for t in range(4):
+                f_matmul(f1_ps[b][:, t, :], t, cb, sb_, b * P, (b + 1) * P)
+        for piece in pieces[:4]:
             silu(piece)
-        cb, sb_ = quant("a1", a_g[1], V)
-        f_product(1, cb, sb_)
-        for t in range(4):
-            fetch(0, t, 0, V)
+        nc.scalar.copy(f1[0][:], f1_ps[0][:])
+        for piece in pieces[4:]:
+            silu(piece)
+        nc.scalar.copy(f1[1][:], f1_ps[1][:])
+        nc.scalar.copy(f0_high[1][:], f0_ps[1][:, 1, P:V])
         for t in range(3):
-            fetch(1, t, 0, V)
-        fetch(1, 3, 0, P)
-        fetch(1, 3, P, V)
-        join(0)
-        finish(0)
+            fetch(0, t, 0, V, f0_low[:, t, :])
+        for t in range(2):
+            fetch(1, t, 0, P, f1[0][:, t, :])
+        turned_sum(0)
+        fetch(1, 2, 0, P, f1[0][:, 2, :])
+        fetch(0, 3, 0, P, f0_high[0][:])
+        fetch(1, 3, 0, P, f1[0][:, 3, :])
+        turned_sum(1)
+        nc.scalar.copy(
+            z_g[0][:].bitcast(F32).rearrange("p (v u) -> p v u", u=2), words_ps[0][:].rearrange("p u v -> p v u")
+        )
+        for t in range(4):
+            fetch(1, t, P, V, f1[1][:, t, :])
+        fetch(0, 3, P, V, f0_high[1][:])
         join(1)
+        finish(0)
         finish(1)

@@ -51,11 +51,6 @@ def tile_picked_dime_silu_p_kernel(
 
         nc.vector.memset(xs[:, :].bitcast(I32), 0)
 
-        warm = tile("warm", [P, 32], F32)
-        nc.vector.memset(warm[:], 0.0)
-        warm2 = tile("warm2", [P, 32], F32)
-        nc.scalar.activation(warm2[:], warm[:], SILU)
-
         ident = tile("ident", [P, P], F32)
         make_identity(nc, ident[:])
 

@@ -1,7 +1,6 @@
 from contextlib import ExitStack
 
 import concourse.mybir as mybir
-from concourse.masks import make_identity
 
 K, T, S, V, H, N, J = 1024, 2048, 512, 256, 512, 256, 512
 FLOPS = 2 * K * H * S + 2 * J * H * 2 * V + 2 * H * N * V
@@ -15,13 +14,14 @@ U8 = mybir.dt.uint8
 FP8X4 = mybir.dt.float8_e4m3fn_x4
 FP4X4 = mybir.dt.float4_e2m1fn_x4
 SILU = mybir.ActivationFunctionType.Silu
+COPY = mybir.ActivationFunctionType.Copy
 MULT = mybir.AluOpType.mult
 ADD = mybir.AluOpType.add
 
 P = 128
 W1A_VECTOR_ROWS = 64
-W3_VECTOR_ROWS = 88
 W1B_VECTOR_ROWS = 88
+LINE = 64
 
 
 def tile_picked_dime_silu_p_kernel(
@@ -41,18 +41,18 @@ def tile_picked_dime_silu_p_kernel(
 
         offs_t = tile("offs_t", [P, S // 16], U16)
         pos_t = [tile("pos1_t", [P, V // 16], U16), tile("pos2_t", [P, V // 16], U16)]
-        w1_raw = [staged("w1_raw0", [P, 4, H], F32, 8192), staged("w1_raw1", [P, 4, H], F32, 31232)]
-        w3_raw = staged("w3_raw", [P, 4, H], F32, 16384)
-        xs = staged("xs", [P, T], U8, 51200)
-        xw = [staged("xw0", [P, T], I32, 40960), staged("xw1", [P, T], I32, 512)]
-        a_raw = [staged("a_raw0", [P, 4, V], F32, 25088), staged("a_raw1", [P, 4, V], F32, 16384)]
-        w2w = staged("w2w", [P, 2 * N], U8, 25088)
-        w2s = staged("w2s", [P, N], U8, 25600)
+        xw = [staged("xw0", [P, T], I32, 0), staged("xw1", [P, T], I32, 8192 - LINE)]
+        w1_raw = [staged("w1_raw0", [P, 4, H], F32, 20480), staged("w1_raw1", [P, 4, H], F32, 45504)]
+        xsg = [tile("xsg0", [P, S], U8), staged("xsg1", [P, S], U8, 28672 - LINE)]
+        w1_g = [staged("w1_g0", [P, 4 * H], BF16, 41408 - LINE), staged("w1_g1", [P, 4 * H], BF16, 37376 - LINE)]
+        w3_raw = staged("w3_raw", [P, 4, H], F32, 29184)
+        a_raw = [staged("a_raw0", [P, 4, V], F32, 53696 - LINE), staged("a_raw1", [P, 4, V], F32, 16320 - LINE)]
+        w2w = staged("w2w", [P, 2 * N], U8, 35328)
+        w2s = staged("w2s", [P, N], U8, 35840)
+        xs = staged("xs", [P, T], U8, 57792)
+        xg = [staged("xg0", [P, S], U32, 59840 - LINE), tile("xg1", [P, S], U32)]
 
         nc.vector.memset(xs[:, :].bitcast(I32), 0)
-
-        ident = tile("ident", [P, P], F32)
-        make_identity(nc, ident[:])
 
         def load_x(z):
             nc.sync.dma_start(xw[z][:], x_words[z].rearrange("p c r -> p (c r)").bitcast(I32))
@@ -70,25 +70,25 @@ def tile_picked_dime_silu_p_kernel(
             src = a_raw[u][:].rearrange("p j (c i) -> p c j i", i=4)[:, c0:c1]
             engine_copy(dst, src)
 
-        def quant(name, grouped, width, at=None):
-            codes = tile(name + "_c", [P, width], U32) if at is None else staged(name + "_c", [P, width], U32, at)
-            scales = tile(name + "_s", [P, width], U8) if at is None else staged(name + "_s", [P, width], U8, at + 4096)
+        def quant(name, grouped, width):
+            codes = tile(name + "_c", [P, width], U32)
+            scales = tile(name + "_s", [P, width], U8)
             nc.vector.quantize_mx(out=codes[:].bitcast(FP8X4), scales=scales[:], in_=grouped[:])
             return codes, scales
 
-        w1_g = [tile("w1_g%d" % z, [P, 4 * H], BF16) for z in range(2)]
         w3_g = tile("w3_g", [P, 4 * H], BF16)
         a_g = [tile("a_g%d" % u, [P, 4 * V], BF16) for u in range(2)]
-        xg = [tile("xg0", [P, S], U32), tile("xg1", [P, S], U32)]
         xs_rows = tile("xs_rows", [P, S], U8)
-        xsg = [tile("xsg0", [P, S], U8), staged("xsg1", [P, S], U8, 8704)]
-        h_ps = [ps.tile([P, S], F32, name="h_ps%d" % t) for t in range(5)]
-        pieces = [(0, 0, 0, S // 2), (4, 0, S // 2, S), (1, 1, 0, S), (2, 2, 0, S), (3, 3, 0, S)]
-        h = [tile("h0", [P, S], F32), tile("h1", [P, S], F32), tile("h2", [P, S], F32), staged("h3", [P, S], F32, 59392 + 1024 - 64)]
-        f0_low = staged("f0_low", [P, 3, V], F32, 31232)
-        f0_high = [staged("f0_high0", [P, P], F32, 34304), staged("f0_high1", [P, P], F32, 63488)]
-        f1 = [tile("f1_%d" % b, [P, 4, P], F32) for b in range(2)]
-        m = [staged("m0", [P, 4, V], F32, 16384), tile("m1", [P, 4, V], F32)]
+        h_ps = [ps.tile([P, S], F32, name="h_ps%d" % t) for t in range(6)]
+        pieces = [(0, 0, 0, S // 2), (1, 1, 0, S // 2), (4, 0, S // 2, S), (5, 1, S // 2, S), (2, 2, 0, S), (3, 3, 0, S)]
+        h = [tile("h%d" % t, [P, S], F32) for t in range(4)]
+        g0 = [tile("g0_low", [P, 2, V], F32), tile("g0_high", [P, 2, V], F32)]
+        g1 = tile("g1", [P, 4, V], F32)
+
+        def picked(u, t):
+            return g1[:, t, :] if u == 1 else g0[t // 2][:, t % 2, :]
+
+        m = [tile("m%d" % u, [P, 4, V], F32) for u in range(2)]
         z_g = [tile("z_g%d" % b, [P, 4 * P], BF16) for b in range(2)]
 
         def h_pass(z, codes, scales, piece):
@@ -111,13 +111,13 @@ def tile_picked_dime_silu_p_kernel(
                     xs_rows[4 * row : 4 * row + 16 : 4, :].bitcast(I32),
                 )
 
-        def f_matmul(dst, t, ac, asc, v0, v1):
+        def filters(dst, t, codes, scales, v0, v1):
             nc.tensor.matmul_mx(
                 out=dst,
                 lhsT=c3[:, t * P : (t + 1) * P].bitcast(FP8X4),
                 lhsT_scale=s3[:, t * P : (t + 1) * P],
-                rhs=ac[:, v0:v1].bitcast(FP8X4),
-                rhs_scale=asc[:, v0:v1],
+                rhs=codes[:, v0:v1].bitcast(FP8X4),
+                rhs_scale=scales[:, v0:v1],
                 start=True,
                 stop=True,
             )
@@ -126,8 +126,11 @@ def tile_picked_dime_silu_p_kernel(
             bank, t, c0, c1 = piece
             nc.scalar.activation(h[t][:, c0:c1], h_ps[bank][:, c0:c1], SILU)
 
-        def fetch(u, t, v0, v1, factor):
-            nc.vector.tensor_tensor(m[u][:, t, v0:v1], h[t][:].indirect(pos_t[u][:, v0 // 16 : v1 // 16]), factor, MULT)
+        def fetch_scalar(u, t, v0, v1):
+            nc.scalar.activation(picked(u, t)[:, v0:v1], h[t][:].indirect(pos_t[u][:, v0 // 16 : v1 // 16]), COPY)
+
+        def fetch_vector(u, t, v0, v1):
+            nc.vector.tensor_copy(picked(u, t)[:, v0:v1], h[t][:].indirect(pos_t[u][:, v0 // 16 : v1 // 16]))
 
         def join(b):
             nc.vector.tensor_tensor(
@@ -137,25 +140,10 @@ def tile_picked_dime_silu_p_kernel(
                 ADD,
             )
 
-        z_turned = tile("z_turned", [P, 2, 2 * P], BF16)
-        words_ps = []
-
-        def turned_sum(pair):
-            sum_ps = ps.tile([P, 2, P], F32, name="sum_ps%d" % pair, tag="h_ps%d" % pair)
-            for e in range(2):
-                for u in range(2):
-                    nc.tensor.matmul(
-                        sum_ps[:, e, :], m[u][:, 2 * pair + e, 0:P], ident[:], start=(u == 0), stop=(u == 1), is_transpose=True
-                    )
-            nc.scalar.copy(z_turned[:, pair, :].rearrange("v (p e) -> v p e", e=2), sum_ps[:].rearrange("v e p -> v p e"))
-            if pair == 0:
-                words_ps.append(ps.tile([P, 2, P], F32, name="words_ps", tag="h_ps2"))
-            nc.tensor.transpose(words_ps[0][:, pair, :], z_turned[:, pair, :].bitcast(F32), ident[:])
-
         def finish(b):
             cz, sz = quant("z%d" % b, z_g[b], P)
             for r in range(2):
-                o_ps = ps.tile([P, P], F32, name="o_ps%d%d" % (b, r), tag=["h_ps3", "h_ps4", "f_ps0", "f_ps1"][2 * b + r])
+                o_ps = ps.tile([P, P], F32, name="o_ps%d%d" % (b, r), tag=["h_ps2", "h_ps3", "h_ps4", "h_ps5"][2 * b + r])
                 nc.tensor.matmul_mx(
                     out=o_ps[:],
                     lhsT=w2w[:, 2 * r * P : 2 * (r + 1) * P].bitcast(FP4X4),
@@ -175,71 +163,61 @@ def tile_picked_dime_silu_p_kernel(
         nc.sync.dma_start(pos_t[1][:], pos2)
         nc.sync.dma_start(xs[0:P:4, :].bitcast(I32), x_scales.rearrange("z q c -> (z q) c").bitcast(I32))
         nc.sync.dma_start(w1_raw[0][:], rows4(w1[0:512, :]))
-        nc.sync.dma_start(w3_raw[:], rows4(w3))
-
-        nc.sync.dma_start(a_raw[0][:], rows4(aT[:, 0:V]))
         nc.sync.dma_start(w1_raw[1][:], rows4(w1[512:1024, :]))
         nc.vector.tensor_copy(xs_rows[:], xs[:].indirect(offs_t[:]))
         place_scales(0)
         nc.vector.tensor_copy(xg[0][:], xw[0][:].bitcast(U32).indirect(offs_t[:]))
+        load_x(1)
 
         deal(nc.vector.tensor_copy, w1_g[0], w1_raw[0], 0, W1A_VECTOR_ROWS)
         deal(nc.scalar.copy, w1_g[0], w1_raw[0], W1A_VECTOR_ROWS, P)
-        load_x(1)
         place_scales(1)
         c0, s0 = quant("w1a", w1_g[0], H)
         for piece in pieces:
             h_pass(0, c0, s0, piece)
-        deal(nc.vector.tensor_copy, w3_g, w3_raw, 0, W3_VECTOR_ROWS)
-        deal(nc.scalar.copy, w3_g, w3_raw, W3_VECTOR_ROWS, P)
+        deal(nc.vector.tensor_copy, w1_g[1], w1_raw[1], 0, W1B_VECTOR_ROWS)
+        deal(nc.scalar.copy, w1_g[1], w1_raw[1], W1B_VECTOR_ROWS, P)
+        nc.sync.dma_start(a_raw[0][:], rows4(aT[:, 0:V]))
+        c1, s1 = quant("w1b", w1_g[1], H)
+        nc.sync.dma_start(w3_raw[:], rows4(w3))
+        for u in range(2):
+            nc.vector.tensor_copy(xg[1][:, u * 256 : (u + 1) * 256], xw[1][:].bitcast(U32).indirect(offs_t[:, 16 * u : 16 * u + 16]))
         nc.sync.dma_start(a_raw[1][:], rows4(aT[:, V : 2 * V]))
-        c3, s3 = quant("w3", w3_g, H)
-        weave(nc.scalar.copy, 0, 0, V // 4)
+        for piece in pieces:
+            h_pass(1, c1, s1, piece)
+        for piece in pieces:
+            silu(piece)
+        weave(nc.vector.tensor_copy, 0, 0, V // 4)
+        fetch_vector(0, 0, 0, V)
+        ca, sa = quant("a0", a_g[0], V)
+        fetch_vector(0, 1, 0, V)
+        deal(nc.vector.tensor_copy, w3_g, w3_raw, 0, P)
         nc.sync.dma_start(w2w[:], w2_words[0])
         for q in range(4):
             nc.sync.dma_start(w2s[32 * q : 32 * q + 4, :].bitcast(I32), w2_scales[0, 4 * q : 4 * q + 4, :].bitcast(I32))
-        ca, sa = quant("a0", a_g[0], V)
-        deal(nc.vector.tensor_copy, w1_g[1], w1_raw[1], 0, W1B_VECTOR_ROWS)
-        deal(nc.scalar.copy, w1_g[1], w1_raw[1], W1B_VECTOR_ROWS, P)
-        f0_ps = [ps.tile([P, 2, V], F32, name="f0_ps%d" % pair, tag="f_ps%d" % pair) for pair in range(2)]
-        for t in range(4):
-            f_matmul(f0_ps[t // 2][:, t % 2, :], t, ca, sa, 0, V)
-        nc.scalar.copy(f0_low[:, 0:2, :], f0_ps[0][:])
-        nc.scalar.copy(f0_low[:, 2, :], f0_ps[1][:, 0, :])
-        nc.scalar.copy(f0_high[0][:], f0_ps[1][:, 1, 0:P])
-        c1, s1 = quant("w1b", w1_g[1], H)
-        for u in range(2):
-            nc.vector.tensor_copy(xg[1][:, u * 256 : (u + 1) * 256], xw[1][:].bitcast(U32).indirect(offs_t[:, 16 * u : 16 * u + 16]))
-        for piece in pieces:
-            h_pass(1, c1, s1, piece)
         weave(nc.vector.tensor_copy, 1, 0, V // 4)
-        cb, sb_ = quant("a1", a_g[1], V, 59392)
-        f1_ps = [ps.tile([P, 4, P], F32, name="f1_ps%d" % b, tag=["f_ps0", "f_ps2"][b]) for b in range(2)]
+        c3 = tile("w3_c", [P, H], U32)
+        s3 = tile("w3_s", [P, H], U8)
+        for half in range(2):
+            cols = slice(half * H // 2, (half + 1) * H // 2)
+            nc.vector.quantize_mx(out=c3[:, cols].bitcast(FP8X4), scales=s3[:, cols], in_=w3_g[:, half * 2 * H : (half + 1) * 2 * H])
+        cb, sb_ = quant("a1", a_g[1], V)
+        f0 = [ps.tile([P, 2, V], F32, name="f0_ps%d" % pair, tag="f_ps%d" % pair) for pair in range(2)]
+        for t in range(4):
+            filters(f0[t // 2][:, t % 2, :], t, ca, sa, 0, V)
+        for t in range(2, 4):
+            fetch_scalar(0, t, 0, V)
+        for t in range(4):
+            fetch_scalar(1, t, 0, V)
+        nc.vector.tensor_tensor(m[0][:, 0:2, :], g0[0][:], f0[0][:], MULT)
+        f1 = [ps.tile([P, 4, P], F32, name="f1_ps%d" % b, tag="h_ps%d" % b) for b in range(2)]
         for b in range(2):
             for t in range(4):
-                f_matmul(f1_ps[b][:, t, :], t, cb, sb_, b * P, (b + 1) * P)
-        for piece in pieces[:4]:
-            silu(piece)
-        nc.scalar.copy(f1[0][:], f1_ps[0][:])
-        for piece in pieces[4:]:
-            silu(piece)
-        nc.scalar.copy(f1[1][:], f1_ps[1][:])
-        nc.scalar.copy(f0_high[1][:], f0_ps[1][:, 1, P:V])
-        for t in range(3):
-            fetch(0, t, 0, V, f0_low[:, t, :])
-        for t in range(2):
-            fetch(1, t, 0, P, f1[0][:, t, :])
-        turned_sum(0)
-        fetch(1, 2, 0, P, f1[0][:, 2, :])
-        fetch(0, 3, 0, P, f0_high[0][:])
-        fetch(1, 3, 0, P, f1[0][:, 3, :])
-        turned_sum(1)
-        nc.scalar.copy(
-            z_g[0][:].bitcast(F32).rearrange("p (v u) -> p v u", u=2), words_ps[0][:].rearrange("p u v -> p v u")
-        )
-        for t in range(4):
-            fetch(1, t, P, V, f1[1][:, t, :])
-        fetch(0, 3, P, V, f0_high[1][:])
+                filters(f1[b][:, t, :], t, cb, sb_, b * P, (b + 1) * P)
+        nc.vector.tensor_tensor(m[0][:, 2:4, :], g0[1][:], f0[1][:], MULT)
+        for b in range(2):
+            nc.vector.tensor_tensor(m[1][:, :, b * P : (b + 1) * P], g1[:, :, b * P : (b + 1) * P], f1[b][:], MULT)
+        join(0)
         join(1)
         finish(0)
         finish(1)

@@ -21,6 +21,7 @@ ADD = mybir.AluOpType.add
 P = 128
 W1A_VECTOR_ROWS = 64
 W1B_VECTOR_ROWS = 88
+W3_SCALAR_ROWS = 32
 LINE = 64
 
 
@@ -45,10 +46,13 @@ def tile_picked_dime_silu_p_kernel(
         w1_raw = [staged("w1_raw0", [P, 4, H], F32, 20480), staged("w1_raw1", [P, 4, H], F32, 45504)]
         xsg = [tile("xsg0", [P, S], U8), staged("xsg1", [P, S], U8, 28672 - LINE)]
         w1_g = [staged("w1_g0", [P, 4 * H], BF16, 41408 - LINE), staged("w1_g1", [P, 4 * H], BF16, 37376 - LINE)]
-        w3_raw = staged("w3_raw", [P, 4, H], F32, 29184)
+        w3_raw = [
+            staged("w3_raw0", [P, 4, 4 * W3_SCALAR_ROWS], F32, 37376 - LINE),
+            staged("w3_raw1", [P, 4, H - 4 * W3_SCALAR_ROWS], F32, 61824 - LINE),
+        ]
         a_raw = [staged("a_raw0", [P, 4, V], F32, 53696 - LINE), staged("a_raw1", [P, 4, V], F32, 16320 - LINE)]
-        w2w = staged("w2w", [P, 2 * N], U8, 35328)
-        w2s = staged("w2s", [P, N], U8, 35840)
+        w2w = staged("w2w", [P, 2 * N], U8, 62464)
+        w2s = staged("w2s", [P, N], U8, 62976)
         xs = staged("xs", [P, T], U8, 57792)
         xg = [staged("xg0", [P, S], U32, 59840 - LINE), tile("xg1", [P, S], U32)]
 
@@ -60,8 +64,8 @@ def tile_picked_dime_silu_p_kernel(
         def rows4(w):
             return w.rearrange("(p j) c -> p j c", j=4)
 
-        def deal(engine_copy, grouped, raw, m0, m1):
-            dst = grouped[:].rearrange("p (t m j) -> p m j t", t=4, j=4)[:, m0:m1]
+        def deal(engine_copy, grouped, raw, m0, m1, first=0):
+            dst = grouped[:].rearrange("p (t m j) -> p m j t", t=4, j=4)[:, first + m0 : first + m1]
             src = raw[:].rearrange("p j (m t) -> p m j t", t=4)[:, m0:m1]
             engine_copy(dst, src)
 
@@ -83,10 +87,10 @@ def tile_picked_dime_silu_p_kernel(
         pieces = [(0, 0, 0, S // 2), (1, 1, 0, S // 2), (4, 0, S // 2, S), (5, 1, S // 2, S), (2, 2, 0, S), (3, 3, 0, S)]
         h = [tile("h%d" % t, [P, S], F32) for t in range(4)]
         g0 = [tile("g0_low", [P, 2, V], F32), tile("g0_high", [P, 2, V], F32)]
-        g1 = tile("g1", [P, 4, V], F32)
+        g1 = [tile("g1_low", [P, 2, V], F32), tile("g1_high", [P, 2, V], F32)]
 
         def picked(u, t):
-            return g1[:, t, :] if u == 1 else g0[t // 2][:, t % 2, :]
+            return [g0, g1][u][t // 2][:, t % 2, :]
 
         m = [tile("m%d" % u, [P, 4, V], F32) for u in range(2)]
         z_g = [tile("z_g%d" % b, [P, 4 * P], BF16) for b in range(2)]
@@ -179,19 +183,23 @@ def tile_picked_dime_silu_p_kernel(
         deal(nc.scalar.copy, w1_g[1], w1_raw[1], W1B_VECTOR_ROWS, P)
         nc.sync.dma_start(a_raw[0][:], rows4(aT[:, 0:V]))
         c1, s1 = quant("w1b", w1_g[1], H)
-        nc.sync.dma_start(w3_raw[:], rows4(w3))
+        nc.sync.dma_start(w3_raw[0][:], rows4(w3[:, 0 : 4 * W3_SCALAR_ROWS]))
+        nc.sync.dma_start(w3_raw[1][:], rows4(w3[:, 4 * W3_SCALAR_ROWS : H]))
         for u in range(2):
             nc.vector.tensor_copy(xg[1][:, u * 256 : (u + 1) * 256], xw[1][:].bitcast(U32).indirect(offs_t[:, 16 * u : 16 * u + 16]))
         nc.sync.dma_start(a_raw[1][:], rows4(aT[:, V : 2 * V]))
         for piece in pieces:
             h_pass(1, c1, s1, piece)
-        for piece in pieces:
+        for piece in pieces[:4]:
+            silu(piece)
+        deal(nc.scalar.copy, w3_g, w3_raw[0], 0, W3_SCALAR_ROWS)
+        for piece in pieces[4:]:
             silu(piece)
         weave(nc.vector.tensor_copy, 0, 0, V // 4)
         fetch_vector(0, 0, 0, V)
         ca, sa = quant("a0", a_g[0], V)
         fetch_vector(0, 1, 0, V)
-        deal(nc.vector.tensor_copy, w3_g, w3_raw, 0, P)
+        deal(nc.vector.tensor_copy, w3_g, w3_raw[1], 0, P - W3_SCALAR_ROWS, W3_SCALAR_ROWS)
         nc.sync.dma_start(w2w[:], w2_words[0])
         for q in range(4):
             nc.sync.dma_start(w2s[32 * q : 32 * q + 4, :].bitcast(I32), w2_scales[0, 4 * q : 4 * q + 4, :].bitcast(I32))
@@ -210,13 +218,14 @@ def tile_picked_dime_silu_p_kernel(
         for t in range(4):
             fetch_scalar(1, t, 0, V)
         nc.vector.tensor_tensor(m[0][:, 0:2, :], g0[0][:], f0[0][:], MULT)
-        f1 = [ps.tile([P, 4, P], F32, name="f1_ps%d" % b, tag="h_ps%d" % b) for b in range(2)]
-        for b in range(2):
-            for t in range(4):
-                filters(f1[b][:, t, :], t, cb, sb_, b * P, (b + 1) * P)
+        f1 = [ps.tile([P, 2, V], F32, name="f1_ps%d" % pair, tag="h_ps%d" % pair) for pair in range(2)]
+        for t in range(4):
+            filters(f1[t // 2][:, t % 2, :], t, cb, sb_, 0, V)
         nc.vector.tensor_tensor(m[0][:, 2:4, :], g0[1][:], f0[1][:], MULT)
+        nc.vector.tensor_tensor(m[1][:, 0:2, :], g1[0][:], f1[0][:], MULT)
         for b in range(2):
-            nc.vector.tensor_tensor(m[1][:, :, b * P : (b + 1) * P], g1[:, :, b * P : (b + 1) * P], f1[b][:], MULT)
+            cols = slice(b * P, (b + 1) * P)
+            nc.vector.tensor_tensor(m[1][:, 2:4, cols], g1[1][:, :, cols], f1[1][:, :, cols], MULT)
         join(0)
         join(1)
         finish(0)

@@ -64,9 +64,9 @@ def tile_picked_dime_silu_p_kernel(
         def rows4(w):
             return w.rearrange("(p j) c -> p j c", j=4)
 
-        def deal(engine_copy, grouped, raw, m0, m1, first=0):
-            dst = grouped[:].rearrange("p (t m j) -> p m j t", t=4, j=4)[:, first + m0 : first + m1]
-            src = raw[:].rearrange("p j (m t) -> p m j t", t=4)[:, m0:m1]
+        def deal(engine_copy, grouped, raw, m0, m1, first=0, t0=0, t1=4):
+            dst = grouped[:].rearrange("p (t m j) -> p m j t", t=4, j=4)[:, first + m0 : first + m1, :, t0:t1]
+            src = raw[:].rearrange("p j (m t) -> p m j t", t=4)[:, m0:m1, :, t0:t1]
             engine_copy(dst, src)
 
         def weave(engine_copy, u, c0, c1):
@@ -87,12 +87,12 @@ def tile_picked_dime_silu_p_kernel(
         pieces = [(0, 0, 0, S // 2), (1, 1, 0, S // 2), (4, 0, S // 2, S), (5, 1, S // 2, S), (2, 2, 0, S), (3, 3, 0, S)]
         h = [tile("h%d" % t, [P, S], F32) for t in range(4)]
         g0 = [tile("g0_low", [P, 2, V], F32), tile("g0_high", [P, 2, V], F32)]
-        g1 = [tile("g1_low", [P, 2, V], F32), tile("g1_high", [P, 2, V], F32)]
+        g1 = tile("g1", [P, 4, V], F32)
 
         def picked(u, t):
-            return [g0, g1][u][t // 2][:, t % 2, :]
+            return g1[:, t, :] if u == 1 else g0[t // 2][:, t % 2, :]
 
-        m = [tile("m%d" % u, [P, 4, V], F32) for u in range(2)]
+        m = [staged("m0", [P, 4, V], F32, 16320 - LINE), tile("m1", [P, 4, V], F32)]
         z_g = [tile("z_g%d" % b, [P, 4 * P], BF16) for b in range(2)]
 
         def h_pass(z, codes, scales, piece):
@@ -164,7 +164,6 @@ def tile_picked_dime_silu_p_kernel(
         load_x(0)
         nc.sync.dma_start(offs_t[:], offs)
         nc.sync.dma_start(pos_t[0][:], pos1)
-        nc.sync.dma_start(pos_t[1][:], pos2)
         nc.sync.dma_start(xs[0:P:4, :].bitcast(I32), x_scales.rearrange("z q c -> (z q) c").bitcast(I32))
         nc.sync.dma_start(w1_raw[0][:], rows4(w1[0:512, :]))
         nc.sync.dma_start(w1_raw[1][:], rows4(w1[512:1024, :]))
@@ -188,6 +187,7 @@ def tile_picked_dime_silu_p_kernel(
         for u in range(2):
             nc.vector.tensor_copy(xg[1][:, u * 256 : (u + 1) * 256], xw[1][:].bitcast(U32).indirect(offs_t[:, 16 * u : 16 * u + 16]))
         nc.sync.dma_start(a_raw[1][:], rows4(aT[:, V : 2 * V]))
+        nc.sync.dma_start(pos_t[1][:], pos2)
         for piece in pieces:
             h_pass(1, c1, s1, piece)
         for piece in pieces[:4]:
@@ -199,33 +199,37 @@ def tile_picked_dime_silu_p_kernel(
         fetch_vector(0, 0, 0, V)
         ca, sa = quant("a0", a_g[0], V)
         fetch_vector(0, 1, 0, V)
-        deal(nc.vector.tensor_copy, w3_g, w3_raw[1], 0, P - W3_SCALAR_ROWS, W3_SCALAR_ROWS)
+        for half in range(2):
+            deal(nc.vector.tensor_copy, w3_g, w3_raw[1], 0, P - W3_SCALAR_ROWS, W3_SCALAR_ROWS, 2 * half, 2 * half + 2)
         nc.sync.dma_start(w2w[:], w2_words[0])
         for q in range(4):
             nc.sync.dma_start(w2s[32 * q : 32 * q + 4, :].bitcast(I32), w2_scales[0, 4 * q : 4 * q + 4, :].bitcast(I32))
-        weave(nc.vector.tensor_copy, 1, 0, V // 4)
         c3 = tile("w3_c", [P, H], U32)
         s3 = tile("w3_s", [P, H], U8)
         for half in range(2):
             cols = slice(half * H // 2, (half + 1) * H // 2)
             nc.vector.quantize_mx(out=c3[:, cols].bitcast(FP8X4), scales=s3[:, cols], in_=w3_g[:, half * 2 * H : (half + 1) * 2 * H])
+            if half == 0:
+                weave(nc.vector.tensor_copy, 1, 0, V // 4)
         cb, sb_ = quant("a1", a_g[1], V)
         f0 = [ps.tile([P, 2, V], F32, name="f0_ps%d" % pair, tag="f_ps%d" % pair) for pair in range(2)]
         for t in range(4):
             filters(f0[t // 2][:, t % 2, :], t, ca, sa, 0, V)
         for t in range(2, 4):
             fetch_scalar(0, t, 0, V)
-        for t in range(4):
+        for t in range(2):
             fetch_scalar(1, t, 0, V)
-        nc.vector.tensor_tensor(m[0][:, 0:2, :], g0[0][:], f0[0][:], MULT)
-        f1 = [ps.tile([P, 2, V], F32, name="f1_ps%d" % pair, tag="h_ps%d" % pair) for pair in range(2)]
-        for t in range(4):
-            filters(f1[t // 2][:, t % 2, :], t, cb, sb_, 0, V)
-        nc.vector.tensor_tensor(m[0][:, 2:4, :], g0[1][:], f0[1][:], MULT)
-        nc.vector.tensor_tensor(m[1][:, 0:2, :], g1[0][:], f1[0][:], MULT)
         for b in range(2):
-            cols = slice(b * P, (b + 1) * P)
-            nc.vector.tensor_tensor(m[1][:, 2:4, cols], g1[1][:, :, cols], f1[1][:, :, cols], MULT)
+            for t in range(2, 4):
+                fetch_scalar(1, t, b * P, (b + 1) * P)
+        nc.vector.tensor_tensor(m[0][:, 0:2, :], g0[0][:], f0[0][:], MULT)
+        f1 = [ps.tile([P, 4, P], F32, name="f1_ps%d" % b, tag="h_ps%d" % b) for b in range(2)]
+        for b in range(2):
+            for t in range(4):
+                filters(f1[b][:, t, :], t, cb, sb_, b * P, (b + 1) * P)
+        nc.vector.tensor_tensor(m[0][:, 2:4, :], g0[1][:], f0[1][:], MULT)
+        for b in range(2):
+            nc.vector.tensor_tensor(m[1][:, :, b * P : (b + 1) * P], g1[:, :, b * P : (b + 1) * P], f1[b][:], MULT)
         join(0)
         join(1)
         finish(0)

@@ -19,10 +19,9 @@ MULT = mybir.AluOpType.mult
 ADD = mybir.AluOpType.add
 
 P = 128
-W1A_VECTOR_ROWS = 64
-W1B_VECTOR_ROWS = 88
-W3_SCALAR_ROWS = 32
-LINE = 64
+W1A_VECTOR_ROWS = 56
+W1B_VECTOR_ROWS = 72
+VECTOR_TARGETS = 192
 
 
 def tile_picked_dime_silu_p_kernel(
@@ -42,19 +41,16 @@ def tile_picked_dime_silu_p_kernel(
 
         offs_t = tile("offs_t", [P, S // 16], U16)
         pos_t = [tile("pos1_t", [P, V // 16], U16), tile("pos2_t", [P, V // 16], U16)]
-        xw = [staged("xw0", [P, T], I32, 0), staged("xw1", [P, T], I32, 8192 - LINE)]
-        w1_raw = [staged("w1_raw0", [P, 4, H], F32, 20480), staged("w1_raw1", [P, 4, H], F32, 45504)]
-        xsg = [tile("xsg0", [P, S], U8), staged("xsg1", [P, S], U8, 28672 - LINE)]
-        w1_g = [staged("w1_g0", [P, 4 * H], BF16, 41408 - LINE), staged("w1_g1", [P, 4 * H], BF16, 37376 - LINE)]
-        w3_raw = [
-            staged("w3_raw0", [P, 4, 4 * W3_SCALAR_ROWS], F32, 37376 - LINE),
-            staged("w3_raw1", [P, 4, H - 4 * W3_SCALAR_ROWS], F32, 61824 - LINE),
-        ]
-        a_raw = [staged("a_raw0", [P, 4, V], F32, 53696 - LINE), staged("a_raw1", [P, 4, V], F32, 16320 - LINE)]
-        w2w = staged("w2w", [P, 2 * N], U8, 62464)
-        w2s = staged("w2s", [P, N], U8, 62976)
-        xs = staged("xs", [P, T], U8, 57792)
-        xg = [staged("xg0", [P, S], U32, 59840 - LINE), tile("xg1", [P, S], U32)]
+        xs = staged("xs", [P, T], U8, 41984)
+        xg = [staged("xg0", [P, S], U32, 40960), tile("xg1", [P, S], U32)]
+        xw = [tile("xw0", [P, T], I32), staged("xw1", [P, T], I32, 43008)]
+        w1_raw = [staged("w1_raw0", [P, 4, H], F32, 8192), staged("w1_raw1", [P, 4, H], F32, 16384)]
+        xsg = [tile("xsg0", [P, S], U8), staged("xsg1", [P, S], U8, 11776)]
+        w1_g = [tile("w1_g0", [P, 4 * H], BF16), staged("w1_g1", [P, 4 * H], BF16, 12288)]
+        a_raw = [staged("a_raw0", [P, 4, V], F32, 7680), staged("a_raw1", [P, 4, V], F32, 38912)]
+        w3_raw = staged("w3_raw", [P, 4, H], F32, 16384)
+        w2w = staged("w2w", [P, 2 * N], U8, 16384)
+        w2s = staged("w2s", [P, N], U8, 16896)
 
         nc.vector.memset(xs[:, :].bitcast(I32), 0)
 
@@ -64,8 +60,8 @@ def tile_picked_dime_silu_p_kernel(
         def rows4(w):
             return w.rearrange("(p j) c -> p j c", j=4)
 
-        def deal(engine_copy, grouped, raw, m0, m1, first=0, t0=0, t1=4):
-            dst = grouped[:].rearrange("p (t m j) -> p m j t", t=4, j=4)[:, first + m0 : first + m1, :, t0:t1]
+        def deal(engine_copy, grouped, raw, m0, m1, t0=0, t1=4):
+            dst = grouped[:].rearrange("p (t m j) -> p m j t", t=4, j=4)[:, m0:m1, :, t0:t1]
             src = raw[:].rearrange("p j (m t) -> p m j t", t=4)[:, m0:m1, :, t0:t1]
             engine_copy(dst, src)
 
@@ -86,13 +82,13 @@ def tile_picked_dime_silu_p_kernel(
         h_ps = [ps.tile([P, S], F32, name="h_ps%d" % t) for t in range(6)]
         pieces = [(0, 0, 0, S // 2), (1, 1, 0, S // 2), (4, 0, S // 2, S), (5, 1, S // 2, S), (2, 2, 0, S), (3, 3, 0, S)]
         h = [tile("h%d" % t, [P, S], F32) for t in range(4)]
-        g0 = [tile("g0_low", [P, 2, V], F32), tile("g0_high", [P, 2, V], F32)]
+        g0 = [staged("g0_low", [P, 2, V], F32, 7680), tile("g0_high", [P, 2, V], F32)]
         g1 = tile("g1", [P, 4, V], F32)
 
         def picked(u, t):
             return g1[:, t, :] if u == 1 else g0[t // 2][:, t % 2, :]
 
-        m = [staged("m0", [P, 4, V], F32, 16320 - LINE), tile("m1", [P, 4, V], F32)]
+        m = [staged("m0", [P, 4, V], F32, 38912), tile("m1", [P, 4, V], F32)]
         z_g = [tile("z_g%d" % b, [P, 4 * P], BF16) for b in range(2)]
 
         def h_pass(z, codes, scales, piece):
@@ -164,43 +160,39 @@ def tile_picked_dime_silu_p_kernel(
         load_x(0)
         nc.sync.dma_start(offs_t[:], offs)
         nc.sync.dma_start(pos_t[0][:], pos1)
+        nc.sync.dma_start(pos_t[1][:], pos2)
         nc.sync.dma_start(xs[0:P:4, :].bitcast(I32), x_scales.rearrange("z q c -> (z q) c").bitcast(I32))
         nc.sync.dma_start(w1_raw[0][:], rows4(w1[0:512, :]))
         nc.sync.dma_start(w1_raw[1][:], rows4(w1[512:1024, :]))
         nc.vector.tensor_copy(xs_rows[:], xs[:].indirect(offs_t[:]))
         place_scales(0)
-        nc.vector.tensor_copy(xg[0][:], xw[0][:].bitcast(U32).indirect(offs_t[:]))
         load_x(1)
+        nc.vector.tensor_copy(xg[0][:], xw[0][:].bitcast(U32).indirect(offs_t[:]))
 
         deal(nc.vector.tensor_copy, w1_g[0], w1_raw[0], 0, W1A_VECTOR_ROWS)
         deal(nc.scalar.copy, w1_g[0], w1_raw[0], W1A_VECTOR_ROWS, P)
         place_scales(1)
+        nc.sync.dma_start(a_raw[0][:], rows4(aT[:, 0:V]))
         c0, s0 = quant("w1a", w1_g[0], H)
         for piece in pieces:
             h_pass(0, c0, s0, piece)
         deal(nc.vector.tensor_copy, w1_g[1], w1_raw[1], 0, W1B_VECTOR_ROWS)
         deal(nc.scalar.copy, w1_g[1], w1_raw[1], W1B_VECTOR_ROWS, P)
-        nc.sync.dma_start(a_raw[0][:], rows4(aT[:, 0:V]))
+        nc.sync.dma_start(w3_raw[:], rows4(w3))
         c1, s1 = quant("w1b", w1_g[1], H)
-        nc.sync.dma_start(w3_raw[0][:], rows4(w3[:, 0 : 4 * W3_SCALAR_ROWS]))
-        nc.sync.dma_start(w3_raw[1][:], rows4(w3[:, 4 * W3_SCALAR_ROWS : H]))
+        nc.sync.dma_start(a_raw[1][:], rows4(aT[:, V : 2 * V]))
         for u in range(2):
             nc.vector.tensor_copy(xg[1][:, u * 256 : (u + 1) * 256], xw[1][:].bitcast(U32).indirect(offs_t[:, 16 * u : 16 * u + 16]))
-        nc.sync.dma_start(a_raw[1][:], rows4(aT[:, V : 2 * V]))
-        nc.sync.dma_start(pos_t[1][:], pos2)
         for piece in pieces:
             h_pass(1, c1, s1, piece)
-        for piece in pieces[:4]:
-            silu(piece)
-        deal(nc.scalar.copy, w3_g, w3_raw[0], 0, W3_SCALAR_ROWS)
-        for piece in pieces[4:]:
+        for piece in pieces:
             silu(piece)
         weave(nc.vector.tensor_copy, 0, 0, V // 4)
-        fetch_vector(0, 0, 0, V)
         ca, sa = quant("a0", a_g[0], V)
-        fetch_vector(0, 1, 0, V)
+        fetch_vector(0, 0, 0, V)
+        fetch_vector(0, 1, 0, VECTOR_TARGETS)
         for half in range(2):
-            deal(nc.vector.tensor_copy, w3_g, w3_raw[1], 0, P - W3_SCALAR_ROWS, W3_SCALAR_ROWS, 2 * half, 2 * half + 2)
+            deal(nc.vector.tensor_copy, w3_g, w3_raw, 0, P, 2 * half, 2 * half + 2)
         nc.sync.dma_start(w2w[:], w2_words[0])
         for q in range(4):
             nc.sync.dma_start(w2s[32 * q : 32 * q + 4, :].bitcast(I32), w2_scales[0, 4 * q : 4 * q + 4, :].bitcast(I32))
@@ -215,6 +207,7 @@ def tile_picked_dime_silu_p_kernel(
         f0 = [ps.tile([P, 2, V], F32, name="f0_ps%d" % pair, tag="f_ps%d" % pair) for pair in range(2)]
         for t in range(4):
             filters(f0[t // 2][:, t % 2, :], t, ca, sa, 0, V)
+        fetch_scalar(0, 1, VECTOR_TARGETS, V)
         for t in range(2, 4):
             fetch_scalar(0, t, 0, V)
         for t in range(2):

@@ -45,14 +45,25 @@ def tile_picked_dime_silu_p_kernel(
         xg = [staged("xg0", [P, S], U32, 40960), tile("xg1", [P, S], U32)]
         xw = [tile("xw0", [P, T], I32), staged("xw1", [P, T], I32, 43008)]
         w1_raw = [staged("w1_raw0", [P, 4, H], F32, 8192), staged("w1_raw1", [P, 4, H], F32, 16384)]
-        xsg = [tile("xsg0", [P, S], U8), staged("xsg1", [P, S], U8, 11776)]
+        xsg = tile("xsg", [P, 2, S], U8)
         w1_g = [tile("w1_g0", [P, 4 * H], BF16), staged("w1_g1", [P, 4 * H], BF16, 12288)]
-        a_raw = [staged("a_raw0", [P, 4, V], F32, 7680), staged("a_raw1", [P, 4, V], F32, 38912)]
-        w3_raw = staged("w3_raw", [P, 4, H], F32, 16384)
-        w2w = staged("w2w", [P, 2 * N], U8, 16384)
-        w2s = staged("w2s", [P, N], U8, 16896)
-
-        nc.vector.memset(xs[:, :].bitcast(I32), 0)
+        a_raw = [staged("a_raw0", [P, 4, V], F32, 7680), staged("a_raw1", [P, 4, V], F32, 12288)]
+        w3_raw = staged("w3_raw", [P, 4, H], F32, 20480)
+        w2w = staged("w2w", [P, 2 * N], U8, 20480)
+        w2s = staged("w2s", [P, N], U8, 20992)
+        xs_rows = tile("xs_rows", [P, S], U8)
+        w3_g = tile("w3_g", [P, 4 * H], BF16)
+        c3 = tile("w3_c", [P, H], U32)
+        s3 = tile("w3_s", [P, H], U8)
+        a_g = [tile("a_g%d" % u, [P, 4 * V], BF16) for u in range(2)]
+        h_first = tile("h_first", [P, S], F32)
+        h_others = tile("h_others", [P, 3, S], F32)
+        h = [h_first[:]] + [h_others[:, t, :] for t in range(3)]
+        g = [staged("g0", [P, 4, V], F32, 7680), tile("g1", [P, 4, V], F32)]
+        m = [staged("m0", [P, 4, V], F32, 12288), tile("m1", [P, 4, V], F32)]
+        z_g = [tile("z_g%d" % b, [P, 4 * P], BF16) for b in range(2)]
+        head_ps = ps.tile([P, 4, P], F32, name="head_ps")
+        rest_ps = [ps.tile([P, S - P], F32, name="rest_ps%d" % t) for t in range(4)]
 
         def load_x(z):
             nc.sync.dma_start(xw[z][:], x_words[z].rearrange("p c r -> p (c r)").bitcast(I32))
@@ -62,13 +73,13 @@ def tile_picked_dime_silu_p_kernel(
 
         def deal(engine_copy, grouped, raw, m0, m1, t0=0, t1=4):
             dst = grouped[:].rearrange("p (t m j) -> p m j t", t=4, j=4)[:, m0:m1, :, t0:t1]
-            src = raw[:].rearrange("p j (m t) -> p m j t", t=4)[:, m0:m1, :, t0:t1]
+            src = raw.rearrange("p j (m t) -> p m j t", t=4)[:, m0:m1, :, t0:t1]
             engine_copy(dst, src)
 
-        def weave(engine_copy, u, c0, c1):
-            dst = a_g[u][:].rearrange("p (c i j) -> p c j i", i=4, j=4)[:, c0:c1]
-            src = a_raw[u][:].rearrange("p j (c i) -> p c j i", i=4)[:, c0:c1]
-            engine_copy(dst, src)
+        def weave(u):
+            dst = a_g[u][:].rearrange("p (c i j) -> p c j i", i=4, j=4)
+            src = a_raw[u][:].rearrange("p j (c i) -> p c j i", i=4)
+            nc.vector.tensor_copy(dst, src)
 
         def quant(name, grouped, width):
             codes = tile(name + "_c", [P, width], U32)
@@ -76,61 +87,44 @@ def tile_picked_dime_silu_p_kernel(
             nc.vector.quantize_mx(out=codes[:].bitcast(FP8X4), scales=scales[:], in_=grouped[:])
             return codes, scales
 
-        w3_g = tile("w3_g", [P, 4 * H], BF16)
-        a_g = [tile("a_g%d" % u, [P, 4 * V], BF16) for u in range(2)]
-        xs_rows = tile("xs_rows", [P, S], U8)
-        h_ps = [ps.tile([P, S], F32, name="h_ps%d" % t) for t in range(6)]
-        pieces = [(0, 0, 0, S // 2), (1, 1, 0, S // 2), (4, 0, S // 2, S), (5, 1, S // 2, S), (2, 2, 0, S), (3, 3, 0, S)]
-        h = [tile("h%d" % t, [P, S], F32) for t in range(4)]
-        g0 = [staged("g0_low", [P, 2, V], F32, 7680), tile("g0_high", [P, 2, V], F32)]
-        g1 = tile("g1", [P, 4, V], F32)
-
-        def picked(u, t):
-            return g1[:, t, :] if u == 1 else g0[t // 2][:, t % 2, :]
-
-        m = [staged("m0", [P, 4, V], F32, 38912), tile("m1", [P, 4, V], F32)]
-        z_g = [tile("z_g%d" % b, [P, 4 * P], BF16) for b in range(2)]
-
-        def h_pass(z, codes, scales, piece):
-            bank, t, c0, c1 = piece
+        def h_matmul(dst, z, codes, scales, t, c0, c1, start, stop):
             nc.tensor.matmul_mx(
-                out=h_ps[bank][:, c0:c1],
+                out=dst,
                 lhsT=codes[:, t * P : (t + 1) * P].bitcast(FP8X4),
                 lhsT_scale=scales[:, t * P : (t + 1) * P],
                 rhs=xg[z][:, c0:c1].bitcast(FP8X4),
-                rhs_scale=xsg[z][:, c0:c1],
-                start=(z == 0),
-                stop=(z == 1),
+                rhs_scale=xsg[:, z, c0:c1],
+                start=start,
+                stop=stop,
             )
 
-        def place_scales(z):
-            for q in range(4):
-                row = 16 * z + 4 * q
-                nc.sync.dma_start(
-                    xsg[z][32 * q : 32 * q + 4, :].bitcast(I32),
-                    xs_rows[4 * row : 4 * row + 16 : 4, :].bitcast(I32),
-                )
+        def h_head(z, codes, scales, t):
+            h_matmul(head_ps[:, t, :], z, codes, scales, t, 0, P, z == 0 and t == 0, z == 1 and t == 3)
 
-        def filters(dst, t, codes, scales, v0, v1):
+        def h_rest(z, codes, scales, t):
+            h_matmul(rest_ps[t][:, 0 : 2 * P], z, codes, scales, t, P, 3 * P, z == 0, False)
+            h_matmul(rest_ps[t][:, 2 * P : 3 * P], z, codes, scales, t, 3 * P, S, False, z == 1)
+
+        def place_scales():
+            for q in range(4):
+                nc.sync.dma_start(xsg[32 * q : 32 * q + 4].bitcast(I32), xs_rows[32 * q : 32 * q + 32 : 4, :].bitcast(I32))
+
+        def fetch_scalar(u, t, v0, v1):
+            nc.scalar.activation(g[u][:, t, v0:v1], h[t].indirect(pos_t[u][:, v0 // 16 : v1 // 16]), COPY)
+
+        def fetch_vector(u, t, v0, v1):
+            nc.vector.tensor_copy(g[u][:, t, v0:v1], h[t].indirect(pos_t[u][:, v0 // 16 : v1 // 16]))
+
+        def filters(dst, t, u, v0, v1):
             nc.tensor.matmul_mx(
                 out=dst,
                 lhsT=c3[:, t * P : (t + 1) * P].bitcast(FP8X4),
                 lhsT_scale=s3[:, t * P : (t + 1) * P],
-                rhs=codes[:, v0:v1].bitcast(FP8X4),
-                rhs_scale=scales[:, v0:v1],
+                rhs=ca[u][0][:, v0:v1].bitcast(FP8X4),
+                rhs_scale=ca[u][1][:, v0:v1],
                 start=True,
                 stop=True,
             )
-
-        def silu(piece):
-            bank, t, c0, c1 = piece
-            nc.scalar.activation(h[t][:, c0:c1], h_ps[bank][:, c0:c1], SILU)
-
-        def fetch_scalar(u, t, v0, v1):
-            nc.scalar.activation(picked(u, t)[:, v0:v1], h[t][:].indirect(pos_t[u][:, v0 // 16 : v1 // 16]), COPY)
-
-        def fetch_vector(u, t, v0, v1):
-            nc.vector.tensor_copy(picked(u, t)[:, v0:v1], h[t][:].indirect(pos_t[u][:, v0 // 16 : v1 // 16]))
 
         def join(b):
             nc.vector.tensor_tensor(
@@ -143,7 +137,7 @@ def tile_picked_dime_silu_p_kernel(
         def finish(b):
             cz, sz = quant("z%d" % b, z_g[b], P)
             for r in range(2):
-                o_ps = ps.tile([P, P], F32, name="o_ps%d%d" % (b, r), tag=["h_ps2", "h_ps3", "h_ps4", "h_ps5"][2 * b + r])
+                o_ps = ps.tile([P, P], F32, name="o_ps%d%d" % (b, r), tag="rest_ps%d" % (2 * b + r))
                 nc.tensor.matmul_mx(
                     out=o_ps[:],
                     lhsT=w2w[:, 2 * r * P : 2 * (r + 1) * P].bitcast(FP4X4),
@@ -157,72 +151,76 @@ def tile_picked_dime_silu_p_kernel(
                 nc.scalar.activation(o[:], o_ps[:], SILU)
                 nc.sync.dma_start(out[r * P : (r + 1) * P, b * P : (b + 1) * P], o[:])
 
+        nc.vector.memset(xs[:, :].bitcast(I32), 0)
         load_x(0)
         nc.sync.dma_start(offs_t[:], offs)
         nc.sync.dma_start(pos_t[0][:], pos1)
         nc.sync.dma_start(pos_t[1][:], pos2)
-        nc.sync.dma_start(xs[0:P:4, :].bitcast(I32), x_scales.rearrange("z q c -> (z q) c").bitcast(I32))
+        nc.sync.dma_start(xs[0:P:4, :].bitcast(I32), x_scales.rearrange("z q c -> q z c").bitcast(I32))
         nc.sync.dma_start(w1_raw[0][:], rows4(w1[0:512, :]))
         nc.sync.dma_start(w1_raw[1][:], rows4(w1[512:1024, :]))
         nc.vector.tensor_copy(xs_rows[:], xs[:].indirect(offs_t[:]))
-        place_scales(0)
+        place_scales()
         load_x(1)
         nc.vector.tensor_copy(xg[0][:], xw[0][:].bitcast(U32).indirect(offs_t[:]))
 
-        deal(nc.vector.tensor_copy, w1_g[0], w1_raw[0], 0, W1A_VECTOR_ROWS)
-        deal(nc.scalar.copy, w1_g[0], w1_raw[0], W1A_VECTOR_ROWS, P)
-        place_scales(1)
+        deal(nc.vector.tensor_copy, w1_g[0], w1_raw[0][:], 0, W1A_VECTOR_ROWS)
+        deal(nc.scalar.copy, w1_g[0], w1_raw[0][:], W1A_VECTOR_ROWS, P)
         nc.sync.dma_start(a_raw[0][:], rows4(aT[:, 0:V]))
         c0, s0 = quant("w1a", w1_g[0], H)
-        for piece in pieces:
-            h_pass(0, c0, s0, piece)
-        deal(nc.vector.tensor_copy, w1_g[1], w1_raw[1], 0, W1B_VECTOR_ROWS)
-        deal(nc.scalar.copy, w1_g[1], w1_raw[1], W1B_VECTOR_ROWS, P)
+        for t in range(4):
+            h_head(0, c0, s0, t)
+            h_rest(0, c0, s0, t)
+        deal(nc.vector.tensor_copy, w1_g[1], w1_raw[1][:], 0, W1B_VECTOR_ROWS)
+        deal(nc.scalar.copy, w1_g[1], w1_raw[1][:], W1B_VECTOR_ROWS, P)
         nc.sync.dma_start(w3_raw[:], rows4(w3))
         c1, s1 = quant("w1b", w1_g[1], H)
         nc.sync.dma_start(a_raw[1][:], rows4(aT[:, V : 2 * V]))
-        for u in range(2):
-            nc.vector.tensor_copy(xg[1][:, u * 256 : (u + 1) * 256], xw[1][:].bitcast(U32).indirect(offs_t[:, 16 * u : 16 * u + 16]))
-        for piece in pieces:
-            h_pass(1, c1, s1, piece)
-        for piece in pieces:
-            silu(piece)
-        weave(nc.vector.tensor_copy, 0, 0, V // 4)
-        ca, sa = quant("a0", a_g[0], V)
+        nc.vector.tensor_copy(xg[1][:, 0:P], xw[1][:].bitcast(U32).indirect(offs_t[:, 0 : P // 16]))
+        nc.vector.tensor_copy(xg[1][:, P:S], xw[1][:].bitcast(U32).indirect(offs_t[:, P // 16 : S // 16]))
+        for t in range(4):
+            h_head(1, c1, s1, t)
+        for t in range(4):
+            h_rest(1, c1, s1, t)
+        nc.scalar.activation(h_first[:, 0:P], head_ps[:, 0, :], SILU)
+        nc.scalar.activation(h_others[:, :, 0:P], head_ps[:, 1:4, :], SILU)
+        for t in range(4):
+            nc.scalar.activation(h[t][:, P:S], rest_ps[t][:], SILU)
+
+        weave(0)
+        ca = [quant("a0", a_g[0], V)]
         fetch_vector(0, 0, 0, V)
-        fetch_vector(0, 1, 0, VECTOR_TARGETS)
+        fetch_vector(1, 0, 0, VECTOR_TARGETS)
         for half in range(2):
-            deal(nc.vector.tensor_copy, w3_g, w3_raw, 0, P, 2 * half, 2 * half + 2)
+            deal(nc.vector.tensor_copy, w3_g, w3_raw[:], 0, P, 2 * half, 2 * half + 2)
         nc.sync.dma_start(w2w[:], w2_words[0])
         for q in range(4):
             nc.sync.dma_start(w2s[32 * q : 32 * q + 4, :].bitcast(I32), w2_scales[0, 4 * q : 4 * q + 4, :].bitcast(I32))
-        c3 = tile("w3_c", [P, H], U32)
-        s3 = tile("w3_s", [P, H], U8)
         for half in range(2):
             cols = slice(half * H // 2, (half + 1) * H // 2)
             nc.vector.quantize_mx(out=c3[:, cols].bitcast(FP8X4), scales=s3[:, cols], in_=w3_g[:, half * 2 * H : (half + 1) * 2 * H])
             if half == 0:
-                weave(nc.vector.tensor_copy, 1, 0, V // 4)
-        cb, sb_ = quant("a1", a_g[1], V)
-        f0 = [ps.tile([P, 2, V], F32, name="f0_ps%d" % pair, tag="f_ps%d" % pair) for pair in range(2)]
-        for t in range(4):
-            filters(f0[t // 2][:, t % 2, :], t, ca, sa, 0, V)
-        fetch_scalar(0, 1, VECTOR_TARGETS, V)
-        for t in range(2, 4):
+                weave(1)
+        ca.append(quant("a1", a_g[1], V))
+        for t in range(1, 4):
             fetch_scalar(0, t, 0, V)
-        for t in range(2):
-            fetch_scalar(1, t, 0, V)
+        fetch_scalar(1, 1, 0, V)
+        fetch_scalar(1, 0, VECTOR_TARGETS, V)
         for b in range(2):
             for t in range(2, 4):
                 fetch_scalar(1, t, b * P, (b + 1) * P)
-        nc.vector.tensor_tensor(m[0][:, 0:2, :], g0[0][:], f0[0][:], MULT)
-        f1 = [ps.tile([P, 4, P], F32, name="f1_ps%d" % b, tag="h_ps%d" % b) for b in range(2)]
+        f0 = [ps.tile([P, 2, V], F32, name="f0_ps%d" % pair) for pair in range(2)]
+        for t in range(4):
+            filters(f0[t // 2][:, t % 2, :], t, 0, 0, V)
+        f1 = [ps.tile([P, 4, P], F32, name="f1_ps%d" % b, tag=["f1_ps0", "head_ps"][b]) for b in range(2)]
         for b in range(2):
             for t in range(4):
-                filters(f1[b][:, t, :], t, cb, sb_, b * P, (b + 1) * P)
-        nc.vector.tensor_tensor(m[0][:, 2:4, :], g0[1][:], f0[1][:], MULT)
+                filters(f1[b][:, t, :], t, 1, b * P, (b + 1) * P)
+        for pair in range(2):
+            nc.vector.tensor_tensor(m[0][:, 2 * pair : 2 * pair + 2, :], g[0][:, 2 * pair : 2 * pair + 2, :], f0[pair][:], MULT)
         for b in range(2):
-            nc.vector.tensor_tensor(m[1][:, :, b * P : (b + 1) * P], g1[:, :, b * P : (b + 1) * P], f1[b][:], MULT)
+            cols = slice(b * P, (b + 1) * P)
+            nc.vector.tensor_tensor(m[1][:, :, cols], g[1][:, :, cols], f1[b][:], MULT)
         join(0)
         join(1)
         finish(0)

@@ -56,14 +56,16 @@ def tile_picked_dime_silu_p_kernel(
         c3 = tile("w3_c", [P, H], U32)
         s3 = tile("w3_s", [P, H], U8)
         a_g = [tile("a_g%d" % u, [P, 4 * V], BF16) for u in range(2)]
-        h_first = tile("h_first", [P, S], F32)
-        h_others = tile("h_others", [P, 3, S], F32)
-        h = [h_first[:]] + [h_others[:, t, :] for t in range(3)]
-        g = [staged("g0", [P, 4, V], F32, 7680), tile("g1", [P, 4, V], F32)]
+        h = [tile("h%d" % t, [P, S], F32) for t in range(4)]
+        g0 = [staged("g0_low", [P, 2, V], F32, 7680), tile("g0_high", [P, 2, V], F32)]
+        g1 = tile("g1", [P, 4, V], F32)
         m = [staged("m0", [P, 4, V], F32, 12288), tile("m1", [P, 4, V], F32)]
         z_g = [tile("z_g%d" % b, [P, 4 * P], BF16) for b in range(2)]
-        head_ps = ps.tile([P, 4, P], F32, name="head_ps")
-        rest_ps = [ps.tile([P, S - P], F32, name="rest_ps%d" % t) for t in range(4)]
+        h_ps = [ps.tile([P, S], F32, name="h_ps%d" % t) for t in range(6)]
+        pieces = [(0, 0, 0, S // 2), (1, 1, 0, S // 2), (4, 0, S // 2, S), (5, 1, S // 2, S), (2, 2, 0, S), (3, 3, 0, S)]
+
+        def picked(u, t):
+            return g1[:, t, :] if u == 1 else g0[t // 2][:, t % 2, :]
 
         def load_x(z):
             nc.sync.dma_start(xw[z][:], x_words[z].rearrange("p c r -> p (c r)").bitcast(I32))
@@ -77,8 +79,8 @@ def tile_picked_dime_silu_p_kernel(
             engine_copy(dst, src)
 
         def weave(u):
-            dst = a_g[u][:].rearrange("p (c i j) -> p c j i", i=4, j=4)
-            src = a_raw[u][:].rearrange("p j (c i) -> p c j i", i=4)
+            dst = a_g[u][:].rearrange("p (c i j) -> p c j i", i=2, j=4)
+            src = a_raw[u][:].rearrange("p j (c i) -> p c j i", i=2)
             nc.vector.tensor_copy(dst, src)
 
         def quant(name, grouped, width):
@@ -87,33 +89,27 @@ def tile_picked_dime_silu_p_kernel(
             nc.vector.quantize_mx(out=codes[:].bitcast(FP8X4), scales=scales[:], in_=grouped[:])
             return codes, scales
 
-        def h_matmul(dst, z, codes, scales, t, c0, c1, start, stop):
+        def h_pass(z, codes, scales, piece):
+            bank, t, c0, c1 = piece
             nc.tensor.matmul_mx(
-                out=dst,
+                out=h_ps[bank][:, c0:c1],
                 lhsT=codes[:, t * P : (t + 1) * P].bitcast(FP8X4),
                 lhsT_scale=scales[:, t * P : (t + 1) * P],
                 rhs=xg[z][:, c0:c1].bitcast(FP8X4),
                 rhs_scale=xsg[:, z, c0:c1],
-                start=start,
-                stop=stop,
+                start=(z == 0),
+                stop=(z == 1),
             )
-
-        def h_head(z, codes, scales, t):
-            h_matmul(head_ps[:, t, :], z, codes, scales, t, 0, P, z == 0 and t == 0, z == 1 and t == 3)
-
-        def h_rest(z, codes, scales, t):
-            h_matmul(rest_ps[t][:, 0 : 2 * P], z, codes, scales, t, P, 3 * P, z == 0, False)
-            h_matmul(rest_ps[t][:, 2 * P : 3 * P], z, codes, scales, t, 3 * P, S, False, z == 1)
 
         def place_scales():
             for q in range(4):
                 nc.sync.dma_start(xsg[32 * q : 32 * q + 4].bitcast(I32), xs_rows[32 * q : 32 * q + 32 : 4, :].bitcast(I32))
 
         def fetch_scalar(u, t, v0, v1):
-            nc.scalar.activation(g[u][:, t, v0:v1], h[t].indirect(pos_t[u][:, v0 // 16 : v1 // 16]), COPY)
+            nc.scalar.activation(picked(u, t)[:, v0:v1], h[t][:].indirect(pos_t[u][:, v0 // 16 : v1 // 16]), COPY)
 
         def fetch_vector(u, t, v0, v1):
-            nc.vector.tensor_copy(g[u][:, t, v0:v1], h[t].indirect(pos_t[u][:, v0 // 16 : v1 // 16]))
+            nc.vector.tensor_copy(picked(u, t)[:, v0:v1], h[t][:].indirect(pos_t[u][:, v0 // 16 : v1 // 16]))
 
         def filters(dst, t, u, v0, v1):
             nc.tensor.matmul_mx(
@@ -128,16 +124,16 @@ def tile_picked_dime_silu_p_kernel(
 
         def join(b):
             nc.vector.tensor_tensor(
-                z_g[b][:].rearrange("p (c i t) -> p c t i", i=4, t=4),
-                m[0][:, :, b * P : (b + 1) * P].rearrange("p t (c i) -> p c t i", i=4),
-                m[1][:, :, b * P : (b + 1) * P].rearrange("p t (c i) -> p c t i", i=4),
+                z_g[b][:].rearrange("p (c i t) -> p c t i", i=2, t=4),
+                m[0][:, :, b * P : (b + 1) * P].rearrange("p t (c i) -> p c t i", i=2),
+                m[1][:, :, b * P : (b + 1) * P].rearrange("p t (c i) -> p c t i", i=2),
                 ADD,
             )
 
         def finish(b):
             cz, sz = quant("z%d" % b, z_g[b], P)
             for r in range(2):
-                o_ps = ps.tile([P, P], F32, name="o_ps%d%d" % (b, r), tag="rest_ps%d" % (2 * b + r))
+                o_ps = ps.tile([P, P], F32, name="o_ps%d%d" % (b, r), tag="h_ps%d" % (2 + 2 * b + r))
                 nc.tensor.matmul_mx(
                     out=o_ps[:],
                     lhsT=w2w[:, 2 * r * P : 2 * (r + 1) * P].bitcast(FP4X4),
@@ -149,13 +145,12 @@ def tile_picked_dime_silu_p_kernel(
                 )
                 o = tile("o%d%d" % (b, r), [P, P], F32)
                 nc.scalar.activation(o[:], o_ps[:], SILU)
-                nc.sync.dma_start(out[r * P : (r + 1) * P, b * P : (b + 1) * P], o[:])
+                [nc.sync, nc.scalar][b * r].dma_start(out[r * P : (r + 1) * P, b * P : (b + 1) * P], o[:])
 
         nc.vector.memset(xs[:, :].bitcast(I32), 0)
         load_x(0)
         nc.sync.dma_start(offs_t[:], offs)
         nc.sync.dma_start(pos_t[0][:], pos1)
-        nc.sync.dma_start(pos_t[1][:], pos2)
         nc.sync.dma_start(xs[0:P:4, :].bitcast(I32), x_scales.rearrange("z q c -> q z c").bitcast(I32))
         nc.sync.dma_start(w1_raw[0][:], rows4(w1[0:512, :]))
         nc.sync.dma_start(w1_raw[1][:], rows4(w1[512:1024, :]))
@@ -168,29 +163,25 @@ def tile_picked_dime_silu_p_kernel(
         deal(nc.scalar.copy, w1_g[0], w1_raw[0][:], W1A_VECTOR_ROWS, P)
         nc.sync.dma_start(a_raw[0][:], rows4(aT[:, 0:V]))
         c0, s0 = quant("w1a", w1_g[0], H)
-        for t in range(4):
-            h_head(0, c0, s0, t)
-            h_rest(0, c0, s0, t)
+        for piece in pieces:
+            h_pass(0, c0, s0, piece)
         deal(nc.vector.tensor_copy, w1_g[1], w1_raw[1][:], 0, W1B_VECTOR_ROWS)
         deal(nc.scalar.copy, w1_g[1], w1_raw[1][:], W1B_VECTOR_ROWS, P)
         nc.sync.dma_start(w3_raw[:], rows4(w3))
+        nc.sync.dma_start(pos_t[1][:], pos2)
         c1, s1 = quant("w1b", w1_g[1], H)
         nc.sync.dma_start(a_raw[1][:], rows4(aT[:, V : 2 * V]))
-        nc.vector.tensor_copy(xg[1][:, 0:P], xw[1][:].bitcast(U32).indirect(offs_t[:, 0 : P // 16]))
-        nc.vector.tensor_copy(xg[1][:, P:S], xw[1][:].bitcast(U32).indirect(offs_t[:, P // 16 : S // 16]))
-        for t in range(4):
-            h_head(1, c1, s1, t)
-        for t in range(4):
-            h_rest(1, c1, s1, t)
-        nc.scalar.activation(h_first[:, 0:P], head_ps[:, 0, :], SILU)
-        nc.scalar.activation(h_others[:, :, 0:P], head_ps[:, 1:4, :], SILU)
-        for t in range(4):
-            nc.scalar.activation(h[t][:, P:S], rest_ps[t][:], SILU)
+        for u in range(2):
+            nc.vector.tensor_copy(xg[1][:, u * 256 : (u + 1) * 256], xw[1][:].bitcast(U32).indirect(offs_t[:, 16 * u : 16 * u + 16]))
+        for piece in pieces:
+            h_pass(1, c1, s1, piece)
+        for bank, t, c0, c1 in pieces:
+            nc.scalar.activation(h[t][:, c0:c1], h_ps[bank][:, c0:c1], SILU)
 
         weave(0)
         ca = [quant("a0", a_g[0], V)]
         fetch_vector(0, 0, 0, V)
-        fetch_vector(1, 0, 0, VECTOR_TARGETS)
+        fetch_vector(0, 1, 0, VECTOR_TARGETS)
         for half in range(2):
             deal(nc.vector.tensor_copy, w3_g, w3_raw[:], 0, P, 2 * half, 2 * half + 2)
         nc.sync.dma_start(w2w[:], w2_words[0])
@@ -202,25 +193,24 @@ def tile_picked_dime_silu_p_kernel(
             if half == 0:
                 weave(1)
         ca.append(quant("a1", a_g[1], V))
-        for t in range(1, 4):
-            fetch_scalar(0, t, 0, V)
-        fetch_scalar(1, 1, 0, V)
-        fetch_scalar(1, 0, VECTOR_TARGETS, V)
+        fetch_scalar(0, 1, VECTOR_TARGETS, V)
+        for u, t in [(0, 2), (0, 3), (1, 0), (1, 1)]:
+            fetch_scalar(u, t, 0, V)
         for b in range(2):
             for t in range(2, 4):
                 fetch_scalar(1, t, b * P, (b + 1) * P)
         f0 = [ps.tile([P, 2, V], F32, name="f0_ps%d" % pair) for pair in range(2)]
         for t in range(4):
             filters(f0[t // 2][:, t % 2, :], t, 0, 0, V)
-        f1 = [ps.tile([P, 4, P], F32, name="f1_ps%d" % b, tag=["f1_ps0", "head_ps"][b]) for b in range(2)]
+        f1 = [ps.tile([P, 4, P], F32, name="f1_ps%d" % b, tag="h_ps%d" % b) for b in range(2)]
         for b in range(2):
             for t in range(4):
                 filters(f1[b][:, t, :], t, 1, b * P, (b + 1) * P)
         for pair in range(2):
-            nc.vector.tensor_tensor(m[0][:, 2 * pair : 2 * pair + 2, :], g[0][:, 2 * pair : 2 * pair + 2, :], f0[pair][:], MULT)
+            nc.vector.tensor_tensor(m[0][:, 2 * pair : 2 * pair + 2, :], g0[pair][:], f0[pair][:], MULT)
         for b in range(2):
             cols = slice(b * P, (b + 1) * P)
-            nc.vector.tensor_tensor(m[1][:, :, cols], g[1][:, :, cols], f1[b][:], MULT)
+            nc.vector.tensor_tensor(m[1][:, :, cols], g1[:, :, cols], f1[b][:], MULT)
         join(0)
         join(1)
         finish(0)

@@ -145,7 +145,7 @@ def tile_picked_dime_silu_p_kernel(
                 )
                 o = tile("o%d%d" % (b, r), [P, P], F32)
                 nc.scalar.activation(o[:], o_ps[:], SILU)
-                [nc.sync, nc.scalar][b * r].dma_start(out[r * P : (r + 1) * P, b * P : (b + 1) * P], o[:])
+                nc.sync.dma_start(out[r * P : (r + 1) * P, b * P : (b + 1) * P], o[:])
 
         nc.vector.memset(xs[:, :].bitcast(I32), 0)
         load_x(0)

@@ -20,8 +20,9 @@ ADD = mybir.AluOpType.add
 
 P = 128
 W1A_VECTOR_ROWS = 56
-W1B_VECTOR_ROWS = 72
+W1B_VECTOR_ROWS = 84
 VECTOR_TARGETS = 192
+A1_VECTOR_COLUMNS = 192
 
 
 def tile_picked_dime_silu_p_kernel(
@@ -78,10 +79,10 @@ def tile_picked_dime_silu_p_kernel(
             src = raw.rearrange("p j (m t) -> p m j t", t=4)[:, m0:m1, :, t0:t1]
             engine_copy(dst, src)
 
-        def weave(u):
-            dst = a_g[u][:].rearrange("p (c i j) -> p c j i", i=2, j=4)
-            src = a_raw[u][:].rearrange("p j (c i) -> p c j i", i=2)
-            nc.vector.tensor_copy(dst, src)
+        def weave(engine_copy, u, c0, c1):
+            dst = a_g[u][:].rearrange("p (c i j) -> p c j i", i=2, j=4)[:, c0 // 2 : c1 // 2]
+            src = a_raw[u][:].rearrange("p j (c i) -> p c j i", i=2)[:, c0 // 2 : c1 // 2]
+            engine_copy(dst, src)
 
         def quant(name, grouped, width):
             codes = tile(name + "_c", [P, width], U32)
@@ -168,9 +169,9 @@ def tile_picked_dime_silu_p_kernel(
         deal(nc.vector.tensor_copy, w1_g[1], w1_raw[1][:], 0, W1B_VECTOR_ROWS)
         deal(nc.scalar.copy, w1_g[1], w1_raw[1][:], W1B_VECTOR_ROWS, P)
         nc.sync.dma_start(w3_raw[:], rows4(w3))
-        nc.sync.dma_start(pos_t[1][:], pos2)
         c1, s1 = quant("w1b", w1_g[1], H)
         nc.sync.dma_start(a_raw[1][:], rows4(aT[:, V : 2 * V]))
+        nc.sync.dma_start(pos_t[1][:], pos2)
         for u in range(2):
             nc.vector.tensor_copy(xg[1][:, u * 256 : (u + 1) * 256], xw[1][:].bitcast(U32).indirect(offs_t[:, 16 * u : 16 * u + 16]))
         for piece in pieces:
@@ -178,7 +179,7 @@ def tile_picked_dime_silu_p_kernel(
         for bank, t, c0, c1 in pieces:
             nc.scalar.activation(h[t][:, c0:c1], h_ps[bank][:, c0:c1], SILU)
 
-        weave(0)
+        weave(nc.vector.tensor_copy, 0, 0, V)
         ca = [quant("a0", a_g[0], V)]
         fetch_vector(0, 0, 0, V)
         fetch_vector(0, 1, 0, VECTOR_TARGETS)
@@ -191,7 +192,8 @@ def tile_picked_dime_silu_p_kernel(
             cols = slice(half * H // 2, (half + 1) * H // 2)
             nc.vector.quantize_mx(out=c3[:, cols].bitcast(FP8X4), scales=s3[:, cols], in_=w3_g[:, half * 2 * H : (half + 1) * 2 * H])
             if half == 0:
-                weave(1)
+                weave(nc.vector.tensor_copy, 1, 0, A1_VECTOR_COLUMNS)
+                weave(nc.scalar.copy, 1, A1_VECTOR_COLUMNS, V)
         ca.append(quant("a1", a_g[1], V))
         fetch_scalar(0, 1, VECTOR_TARGETS, V)
         for u, t in [(0, 2), (0, 3), (1, 0), (1, 1)]:

@@ -21,8 +21,7 @@ ADD = mybir.AluOpType.add
 P = 128
 W1A_VECTOR_ROWS = 56
 W1B_VECTOR_ROWS = 84
-VECTOR_TARGETS = 192
-A1_VECTOR_COLUMNS = 192
+A1_VECTOR_COLUMNS = 160
 
 
 def tile_picked_dime_silu_p_kernel(
@@ -181,8 +180,8 @@ def tile_picked_dime_silu_p_kernel(
 
         weave(nc.vector.tensor_copy, 0, 0, V)
         ca = [quant("a0", a_g[0], V)]
-        fetch_vector(0, 0, 0, V)
-        fetch_vector(0, 1, 0, VECTOR_TARGETS)
+        for t in range(2):
+            fetch_vector(0, t, 0, V)
         for half in range(2):
             deal(nc.vector.tensor_copy, w3_g, w3_raw[:], 0, P, 2 * half, 2 * half + 2)
         nc.sync.dma_start(w2w[:], w2_words[0])
@@ -195,24 +194,20 @@ def tile_picked_dime_silu_p_kernel(
                 weave(nc.vector.tensor_copy, 1, 0, A1_VECTOR_COLUMNS)
                 weave(nc.scalar.copy, 1, A1_VECTOR_COLUMNS, V)
         ca.append(quant("a1", a_g[1], V))
-        fetch_scalar(0, 1, VECTOR_TARGETS, V)
-        for u, t in [(0, 2), (0, 3), (1, 0), (1, 1)]:
+        for u, t in [(0, 2), (0, 3), (1, 0), (1, 1), (1, 2)]:
             fetch_scalar(u, t, 0, V)
         for b in range(2):
-            for t in range(2, 4):
-                fetch_scalar(1, t, b * P, (b + 1) * P)
-        f0 = [ps.tile([P, 2, V], F32, name="f0_ps%d" % pair) for pair in range(2)]
-        for t in range(4):
-            filters(f0[t // 2][:, t % 2, :], t, 0, 0, V)
-        f1 = [ps.tile([P, 4, P], F32, name="f1_ps%d" % b, tag="h_ps%d" % b) for b in range(2)]
-        for b in range(2):
+            fetch_scalar(1, 3, b * P, (b + 1) * P)
+        f = [[ps.tile([P, 2, V], F32, name="f_ps%d%d" % (u, pair), tag=["f_ps%d", "h_ps%d"][u] % pair) for pair in range(2)] for u in range(2)]
+        for u in range(2):
             for t in range(4):
-                filters(f1[b][:, t, :], t, 1, b * P, (b + 1) * P)
+                filters(f[u][t // 2][:, t % 2, :], t, u, 0, V)
         for pair in range(2):
-            nc.vector.tensor_tensor(m[0][:, 2 * pair : 2 * pair + 2, :], g0[pair][:], f0[pair][:], MULT)
+            nc.vector.tensor_tensor(m[0][:, 2 * pair : 2 * pair + 2, :], g0[pair][:], f[0][pair][:], MULT)
+        nc.vector.tensor_tensor(m[1][:, 0:2, :], g1[:, 0:2, :], f[1][0][:], MULT)
         for b in range(2):
             cols = slice(b * P, (b + 1) * P)
-            nc.vector.tensor_tensor(m[1][:, :, cols], g1[:, :, cols], f1[b][:], MULT)
+            nc.vector.tensor_tensor(m[1][:, 2:4, cols], g1[:, 2:4, cols], f[1][1][:, :, cols], MULT)
         join(0)
         join(1)
         finish(0)

@@ -21,7 +21,7 @@ ADD = mybir.AluOpType.add
 P = 128
 W1A_VECTOR_ROWS = 56
 W1B_VECTOR_ROWS = 84
-A1_VECTOR_COLUMNS = 160
+A1_VECTOR_COLUMNS = 128
 
 
 def tile_picked_dime_silu_p_kernel(
@@ -150,7 +150,6 @@ def tile_picked_dime_silu_p_kernel(
         nc.vector.memset(xs[:, :].bitcast(I32), 0)
         load_x(0)
         nc.sync.dma_start(offs_t[:], offs)
-        nc.sync.dma_start(pos_t[0][:], pos1)
         nc.sync.dma_start(xs[0:P:4, :].bitcast(I32), x_scales.rearrange("z q c -> q z c").bitcast(I32))
         nc.sync.dma_start(w1_raw[0][:], rows4(w1[0:512, :]))
         nc.sync.dma_start(w1_raw[1][:], rows4(w1[512:1024, :]))
@@ -162,6 +161,7 @@ def tile_picked_dime_silu_p_kernel(
         deal(nc.vector.tensor_copy, w1_g[0], w1_raw[0][:], 0, W1A_VECTOR_ROWS)
         deal(nc.scalar.copy, w1_g[0], w1_raw[0][:], W1A_VECTOR_ROWS, P)
         nc.sync.dma_start(a_raw[0][:], rows4(aT[:, 0:V]))
+        nc.sync.dma_start(pos_t[0][:], pos1)
         c0, s0 = quant("w1a", w1_g[0], H)
         for piece in pieces:
             h_pass(0, c0, s0, piece)
@@ -180,8 +180,8 @@ def tile_picked_dime_silu_p_kernel(
 
         weave(nc.vector.tensor_copy, 0, 0, V)
         ca = [quant("a0", a_g[0], V)]
-        for t in range(2):
-            fetch_vector(0, t, 0, V)
+        fetch_vector(0, 0, 0, V)
+        fetch_vector(0, 1, 0, P)
         for half in range(2):
             deal(nc.vector.tensor_copy, w3_g, w3_raw[:], 0, P, 2 * half, 2 * half + 2)
         nc.sync.dma_start(w2w[:], w2_words[0])
@@ -194,6 +194,7 @@ def tile_picked_dime_silu_p_kernel(
                 weave(nc.vector.tensor_copy, 1, 0, A1_VECTOR_COLUMNS)
                 weave(nc.scalar.copy, 1, A1_VECTOR_COLUMNS, V)
         ca.append(quant("a1", a_g[1], V))
+        fetch_scalar(0, 1, P, V)
         for u, t in [(0, 2), (0, 3), (1, 0), (1, 1), (1, 2)]:
             fetch_scalar(u, t, 0, V)
         for b in range(2):

@@ -124,9 +124,9 @@ def tile_picked_dime_silu_p_kernel(
 
         def join(b):
             nc.vector.tensor_tensor(
-                z_g[b][:].rearrange("p (c i t) -> p c t i", i=2, t=4),
-                m[0][:, :, b * P : (b + 1) * P].rearrange("p t (c i) -> p c t i", i=2),
-                m[1][:, :, b * P : (b + 1) * P].rearrange("p t (c i) -> p c t i", i=2),
+                z_g[b][:].rearrange("p (c i t) -> p c t i", i=4, t=4),
+                m[0][:, :, b * P : (b + 1) * P].rearrange("p t (c i) -> p c t i", i=4),
+                m[1][:, :, b * P : (b + 1) * P].rearrange("p t (c i) -> p c t i", i=4),
                 ADD,
             )
 

@@ -21,7 +21,7 @@ ADD = mybir.AluOpType.add
 P = 128
 W1A_VECTOR_ROWS = 56
 W1B_VECTOR_ROWS = 84
-A1_VECTOR_COLUMNS = 128
+A1_VECTOR_COLUMNS = 64
 
 
 def tile_picked_dime_silu_p_kernel(
@@ -178,10 +178,16 @@ def tile_picked_dime_silu_p_kernel(
         for bank, t, c0, c1 in pieces:
             nc.scalar.activation(h[t][:, c0:c1], h_ps[bank][:, c0:c1], SILU)
 
-        weave(nc.vector.tensor_copy, 0, 0, V)
-        ca = [quant("a0", a_g[0], V)]
-        fetch_vector(0, 0, 0, V)
-        fetch_vector(0, 1, 0, P)
+        for half in range(2):
+            weave(nc.vector.tensor_copy, 0, half * P, (half + 1) * P)
+        ca = [(tile("a0_c", [P, V], U32), tile("a0_s", [P, V], U8))]
+        for half in range(2):
+            cols = slice(half * P, (half + 1) * P)
+            nc.vector.quantize_mx(out=ca[0][0][:, cols].bitcast(FP8X4), scales=ca[0][1][:, cols], in_=a_g[0][:, half * 4 * P : (half + 1) * 4 * P])
+        for t in range(2):
+            fetch_vector(0, t, 0, V)
+        for t in range(2, 4):
+            fetch_scalar(0, t, 0, V)
         for half in range(2):
             deal(nc.vector.tensor_copy, w3_g, w3_raw[:], 0, P, 2 * half, 2 * half + 2)
         nc.sync.dma_start(w2w[:], w2_words[0])
@@ -194,9 +200,8 @@ def tile_picked_dime_silu_p_kernel(
                 weave(nc.vector.tensor_copy, 1, 0, A1_VECTOR_COLUMNS)
                 weave(nc.scalar.copy, 1, A1_VECTOR_COLUMNS, V)
         ca.append(quant("a1", a_g[1], V))
-        fetch_scalar(0, 1, P, V)
-        for u, t in [(0, 2), (0, 3), (1, 0), (1, 1), (1, 2)]:
-            fetch_scalar(u, t, 0, V)
+        for t in range(3):
+            fetch_scalar(1, t, 0, V)
         for b in range(2):
             fetch_scalar(1, 3, b * P, (b + 1) * P)
         f = [[ps.tile([P, 2, V], F32, name="f_ps%d%d" % (u, pair), tag=["f_ps%d", "h_ps%d"][u] % pair) for pair in range(2)] for u in range(2)]

from contextlib import ExitStack

import concourse.mybir as mybir

K, T, S, V, H, N, J = 1024, 2048, 512, 256, 512, 256, 512
FLOPS = 2 * K * H * S + 2 * J * H * 2 * V + 2 * H * N * V

F32 = mybir.dt.float32
BF16 = mybir.dt.bfloat16
I32 = mybir.dt.int32
U32 = mybir.dt.uint32
U16 = mybir.dt.uint16
U8 = mybir.dt.uint8
FP8X4 = mybir.dt.float8_e4m3fn_x4
FP4X4 = mybir.dt.float4_e2m1fn_x4
SILU = mybir.ActivationFunctionType.Silu
COPY = mybir.ActivationFunctionType.Copy
MULT = mybir.AluOpType.mult
ADD = mybir.AluOpType.add

P = 128
W1A_VECTOR_ROWS = 56
W1B_VECTOR_ROWS = 84
A1_VECTOR_COLUMNS = 64


def tile_picked_dime_silu_p_kernel(
    tc, x_words, x_scales, aT, w1, w3, w2_words, w2_scales, offs, pos1, pos2, out
):
    nc = tc.nc
    with ExitStack() as ctx:
        sb = ctx.enter_context(tc.tile_pool(name="sb", bufs=1))
        stage = ctx.enter_context(tc.tile_pool(name="stage", bufs=1))
        ps = ctx.enter_context(tc.psum_pool(name="ps", bufs=1))

        def tile(name, shape, dtype):
            return sb.tile(shape, dtype, name=name, align_bytes=64)

        def staged(name, shape, dtype, offset):
            return stage.tile(shape, dtype, name=name, align_bytes=64, offset=offset)

        offs_t = tile("offs_t", [P, S // 16], U16)
        pos_t = [tile("pos1_t", [P, V // 16], U16), tile("pos2_t", [P, V // 16], U16)]
        xs = staged("xs", [P, T], U8, 41984)
        xg = [staged("xg0", [P, S], U32, 40960), tile("xg1", [P, S], U32)]
        xw = [tile("xw0", [P, T], I32), staged("xw1", [P, T], I32, 43008)]
        w1_raw = [staged("w1_raw0", [P, 4, H], F32, 8192), staged("w1_raw1", [P, 4, H], F32, 16384)]
        xsg = tile("xsg", [P, 2, S], U8)
        w1_g = [tile("w1_g0", [P, 4 * H], BF16), staged("w1_g1", [P, 4 * H], BF16, 12288)]
        a_raw = [staged("a_raw0", [P, 4, V], F32, 7680), staged("a_raw1", [P, 4, V], F32, 12288)]
        w3_raw = staged("w3_raw", [P, 4, H], F32, 20480)
        w2w = staged("w2w", [P, 2 * N], U8, 20480)
        w2s = staged("w2s", [P, N], U8, 20992)
        xs_rows = tile("xs_rows", [P, S], U8)
        w3_g = tile("w3_g", [P, 4 * H], BF16)
        c3 = tile("w3_c", [P, H], U32)
        s3 = tile("w3_s", [P, H], U8)
        a_g = [tile("a_g%d" % u, [P, 4 * V], BF16) for u in range(2)]
        h = [tile("h%d" % t, [P, S], F32) for t in range(4)]
        g0 = [staged("g0_low", [P, 2, V], F32, 7680), tile("g0_high", [P, 2, V], F32)]
        g1 = tile("g1", [P, 4, V], F32)
        m = [staged("m0", [P, 4, V], F32, 12288), tile("m1", [P, 4, V], F32)]
        z_g = [tile("z_g%d" % b, [P, 4 * P], BF16) for b in range(2)]
        h_ps = [ps.tile([P, S], F32, name="h_ps%d" % t) for t in range(6)]
        pieces = [(0, 0, 0, S // 2), (1, 1, 0, S // 2), (4, 0, S // 2, S), (5, 1, S // 2, S), (2, 2, 0, S), (3, 3, 0, S)]

        def picked(u, t):
            return g1[:, t, :] if u == 1 else g0[t // 2][:, t % 2, :]

        def load_x(z):
            nc.sync.dma_start(xw[z][:], x_words[z].rearrange("p c r -> p (c r)").bitcast(I32))

        def rows4(w):
            return w.rearrange("(p j) c -> p j c", j=4)

        def deal(engine_copy, grouped, raw, m0, m1, t0=0, t1=4):
            dst = grouped[:].rearrange("p (t m j) -> p m j t", t=4, j=4)[:, m0:m1, :, t0:t1]
            src = raw.rearrange("p j (m t) -> p m j t", t=4)[:, m0:m1, :, t0:t1]
            engine_copy(dst, src)

        def weave(engine_copy, u, c0, c1):
            dst = a_g[u][:].rearrange("p (c i j) -> p c j i", i=2, j=4)[:, c0 // 2 : c1 // 2]
            src = a_raw[u][:].rearrange("p j (c i) -> p c j i", i=2)[:, c0 // 2 : c1 // 2]
            engine_copy(dst, src)

        def quant(name, grouped, width):
            codes = tile(name + "_c", [P, width], U32)
            scales = tile(name + "_s", [P, width], U8)
            nc.vector.quantize_mx(out=codes[:].bitcast(FP8X4), scales=scales[:], in_=grouped[:])
            return codes, scales

        def h_pass(z, codes, scales, piece):
            bank, t, c0, c1 = piece
            nc.tensor.matmul_mx(
                out=h_ps[bank][:, c0:c1],
                lhsT=codes[:, t * P : (t + 1) * P].bitcast(FP8X4),
                lhsT_scale=scales[:, t * P : (t + 1) * P],
                rhs=xg[z][:, c0:c1].bitcast(FP8X4),
                rhs_scale=xsg[:, z, c0:c1],
                start=(z == 0),
                stop=(z == 1),
            )

        def place_scales():
            for q in range(4):
                nc.sync.dma_start(xsg[32 * q : 32 * q + 4].bitcast(I32), xs_rows[32 * q : 32 * q + 32 : 4, :].bitcast(I32))

        def fetch_scalar(u, t, v0, v1):
            nc.scalar.activation(picked(u, t)[:, v0:v1], h[t][:].indirect(pos_t[u][:, v0 // 16 : v1 // 16]), COPY)

        def fetch_vector(u, t, v0, v1):
            nc.vector.tensor_copy(picked(u, t)[:, v0:v1], h[t][:].indirect(pos_t[u][:, v0 // 16 : v1 // 16]))

        def filters(dst, t, u, v0, v1):
            nc.tensor.matmul_mx(
                out=dst,
                lhsT=c3[:, t * P : (t + 1) * P].bitcast(FP8X4),
                lhsT_scale=s3[:, t * P : (t + 1) * P],
                rhs=ca[u][0][:, v0:v1].bitcast(FP8X4),
                rhs_scale=ca[u][1][:, v0:v1],
                start=True,
                stop=True,
            )

        def join(b):
            nc.vector.tensor_tensor(
                z_g[b][:].rearrange("p (c i t) -> p c t i", i=4, t=4),
                m[0][:, :, b * P : (b + 1) * P].rearrange("p t (c i) -> p c t i", i=4),
                m[1][:, :, b * P : (b + 1) * P].rearrange("p t (c i) -> p c t i", i=4),
                ADD,
            )

        def finish(b):
            cz, sz = quant("z%d" % b, z_g[b], P)
            for r in range(2):
                o_ps = ps.tile([P, P], F32, name="o_ps%d%d" % (b, r), tag="h_ps%d" % (2 + 2 * b + r))
                nc.tensor.matmul_mx(
                    out=o_ps[:],
                    lhsT=w2w[:, 2 * r * P : 2 * (r + 1) * P].bitcast(FP4X4),
                    lhsT_scale=w2s[:, r * P : (r + 1) * P],
                    rhs=cz[:].bitcast(FP8X4),
                    rhs_scale=sz[:],
                    start=True,
                    stop=True,
                )
                o = tile("o%d%d" % (b, r), [P, P], F32)
                nc.scalar.activation(o[:], o_ps[:], SILU)
                nc.sync.dma_start(out[r * P : (r + 1) * P, b * P : (b + 1) * P], o[:])

        nc.vector.memset(xs[:, :].bitcast(I32), 0)
        load_x(0)
        nc.sync.dma_start(offs_t[:], offs)
        nc.sync.dma_start(xs[0:P:4, :].bitcast(I32), x_scales.rearrange("z q c -> q z c").bitcast(I32))
        nc.sync.dma_start(w1_raw[0][:], rows4(w1[0:512, :]))
        nc.sync.dma_start(w1_raw[1][:], rows4(w1[512:1024, :]))
        nc.vector.tensor_copy(xs_rows[:], xs[:].indirect(offs_t[:]))
        place_scales()
        load_x(1)
        nc.vector.tensor_copy(xg[0][:], xw[0][:].bitcast(U32).indirect(offs_t[:]))

        deal(nc.vector.tensor_copy, w1_g[0], w1_raw[0][:], 0, W1A_VECTOR_ROWS)
        deal(nc.scalar.copy, w1_g[0], w1_raw[0][:], W1A_VECTOR_ROWS, P)
        nc.sync.dma_start(a_raw[0][:], rows4(aT[:, 0:V]))
        nc.sync.dma_start(pos_t[0][:], pos1)
        c0, s0 = quant("w1a", w1_g[0], H)
        for piece in pieces:
            h_pass(0, c0, s0, piece)
        deal(nc.vector.tensor_copy, w1_g[1], w1_raw[1][:], 0, W1B_VECTOR_ROWS)
        deal(nc.scalar.copy, w1_g[1], w1_raw[1][:], W1B_VECTOR_ROWS, P)
        nc.sync.dma_start(w3_raw[:], rows4(w3))
        c1, s1 = quant("w1b", w1_g[1], H)
        nc.sync.dma_start(a_raw[1][:], rows4(aT[:, V : 2 * V]))
        nc.sync.dma_start(pos_t[1][:], pos2)
        for u in range(2):
            nc.vector.tensor_copy(xg[1][:, u * 256 : (u + 1) * 256], xw[1][:].bitcast(U32).indirect(offs_t[:, 16 * u : 16 * u + 16]))
        for piece in pieces:
            h_pass(1, c1, s1, piece)
        for bank, t, c0, c1 in pieces:
            nc.scalar.activation(h[t][:, c0:c1], h_ps[bank][:, c0:c1], SILU)

        for half in range(2):
            weave(nc.vector.tensor_copy, 0, half * P, (half + 1) * P)
        ca = [(tile("a0_c", [P, V], U32), tile("a0_s", [P, V], U8))]
        for half in range(2):
            cols = slice(half * P, (half + 1) * P)
            nc.vector.quantize_mx(out=ca[0][0][:, cols].bitcast(FP8X4), scales=ca[0][1][:, cols], in_=a_g[0][:, half * 4 * P : (half + 1) * 4 * P])
        for t in range(2):
            fetch_vector(0, t, 0, V)
        for t in range(2, 4):
            fetch_scalar(0, t, 0, V)
        for half in range(2):
            deal(nc.vector.tensor_copy, w3_g, w3_raw[:], 0, P, 2 * half, 2 * half + 2)
        nc.sync.dma_start(w2w[:], w2_words[0])
        for q in range(4):
            nc.sync.dma_start(w2s[32 * q : 32 * q + 4, :].bitcast(I32), w2_scales[0, 4 * q : 4 * q + 4, :].bitcast(I32))
        for half in range(2):
            cols = slice(half * H // 2, (half + 1) * H // 2)
            nc.vector.quantize_mx(out=c3[:, cols].bitcast(FP8X4), scales=s3[:, cols], in_=w3_g[:, half * 2 * H : (half + 1) * 2 * H])
            if half == 0:
                weave(nc.vector.tensor_copy, 1, 0, A1_VECTOR_COLUMNS)
                weave(nc.scalar.copy, 1, A1_VECTOR_COLUMNS, V)
        ca.append(quant("a1", a_g[1], V))
        for t in range(3):
            fetch_scalar(1, t, 0, V)
        for b in range(2):
            fetch_scalar(1, 3, b * P, (b + 1) * P)
        f = [[ps.tile([P, 2, V], F32, name="f_ps%d%d" % (u, pair), tag=["f_ps%d", "h_ps%d"][u] % pair) for pair in range(2)] for u in range(2)]
        for u in range(2):
            for t in range(4):
                filters(f[u][t // 2][:, t % 2, :], t, u, 0, V)
        for pair in range(2):
            nc.vector.tensor_tensor(m[0][:, 2 * pair : 2 * pair + 2, :], g0[pair][:], f[0][pair][:], MULT)
        nc.vector.tensor_tensor(m[1][:, 0:2, :], g1[:, 0:2, :], f[1][0][:], MULT)
        for b in range(2):
            cols = slice(b * P, (b + 1) * P)
            nc.vector.tensor_tensor(m[1][:, 2:4, cols], g1[:, 2:4, cols], f[1][1][:, :, cols], MULT)
        join(0)
        join(1)
        finish(0)
        finish(1)
